import numpy as np, ml_dtypes
CORES = [35,38,43,46]
N = 4
BF = ml_dtypes.bfloat16
M, C, W, RO = 256, 16, 4096, 6
TOP = 255 * N * C
def settle(rng, e):
    x = np.add.accumulate(e, axis=3); x = x - np.min(x, axis=3, keepdims=True); top = np.max(x, axis=3, keepdims=True)
    return x + 32 + (rng.random(top.shape) * (169 - top)).astype(np.int64)
def parts(rng):
    e = rng.integers(-3, 4, (8, 16, M, 8)); x = settle(rng, rng.permuted(np.concatenate([e, -e], axis=3), axis=3))
    s = np.argsort(rng.random((8, 16, M)), axis=1); miss = rng.integers(0, 16, (8, M))
    u = N * C * 127 + rng.integers(-600, 601, (8, 16, M))
    return x, s, miss, u, rng.integers(0, 256, (N, 8, 16, W)), rng.integers(0, 128, (N, 8, 16, C))
def pack(x, s, miss, u, d, a):
    n = np.where(np.arange(16)[:, None] == miss[:, None, :], -1, s)
    def same(y): return np.repeat(np.ascontiguousarray(y).reshape(1, 128, -1), N, axis=0)
    return {"v": same(x).astype(np.float32).astype(BF), "inv": same(n).astype(np.int32), "sup": same(u).astype(np.int32),
            "dem": d.reshape(N, 128, W).astype(np.float32).astype(BF), "wt": np.ascontiguousarray(a).reshape(N, 128, C).astype(np.float32).astype(BF)}
def newcomer(s, miss):
    return np.take_along_axis(s, miss[:, None, :], 1)[:, 0]
def climb(rng, x, s, miss, u, d, a, g):
    o = rng.permutation(16); turn = rng.integers(0, 16, M); j = (np.arange(16) - turn[:, None]) % 16
    key = int(rng.integers(0, 16)); b = int(rng.integers(32, 177))
    far = np.where(rng.random((16, M, 1)) < 0.5, 32 + 3 * (j & 1), 200 - 3 * (j & 1))
    x[g] = np.where(rng.random((16, M, 1)) < 0.5, far, x[g]); x[g, key] = b + 3 * np.minimum(j, 16 - j)
    t = np.zeros((16, M), np.int64); t[o[:5]] = np.arange(1, 6)[:, None]
    t[o[5:]] = rng.permuted(np.repeat(np.array([0, 6, 7, 8, 9, 10, 11, 12, 13, 14, 15])[:, None], M, axis=1), axis=0)
    s[g] = (t + turn) % 16; miss[g] = np.argmax(t == 8, axis=0)
    u[g] = rng.integers(0, 128 * N * C, (16, M)); d[:, g] = rng.integers(0, 64, (N, 16, W)); a[:, g] = 0; a[:, g, key] = 1
    at = [-1] + [int(y) for y in o[:5]] + [-1] * 10; c = 8
    for w in [int(y) for y in rng.permutation(np.array([1, 3, 5]))] + [int(y) for y in rng.permutation(np.array([2, 4]))] + [3]:
        d[:, g, at[w], b + 3 * c] = 255; at[c] = at[w]; c = w
def setup_inputs(rng):
    return pack(*parts(rng))
def setup_inputs_alike(rng):
    x, s, miss, u, d, a = parts(rng)
    for g in (0, 2, 5, 7): x[g] = x[g][:, :1]; s[g] = s[g][:, :1]; miss[g] = miss[g, 0]; u[g] = u[g][:, :1]
    for g in (1, 2, 6, 7): a[:, g] = a[:, g, :, :1]
    for y in (d, a): y[:, 3] = y[:1, 3].copy(); y[1, 4] = y[0, 4]
    return pack(x, s, miss, u, d, a)
def setup_inputs_ends(rng):
    x, s, miss, u, d, a = parts(rng)
    e = rng.permuted(np.broadcast_to(np.repeat(np.array([3, -3]), 8), (8, 16, M, 16)).copy(), axis=3); e[:, ::2] = np.sort(e[:, ::2], axis=3)
    x = np.add.accumulate(e, axis=3); x = x - np.min(x, axis=3, keepdims=True); top = np.max(x, axis=3, keepdims=True)
    low = rng.random(top.shape) < 0.5; low[3] = False
    x = x + np.where(low, 32, 200 - top); c = newcomer(s, miss)
    for g in range(8):
        for i in (14, 15): x[g, i, 0] += 50 + i - x[g, i, 0, c[g, 0]]
    a = 127 * rng.integers(0, 2, a.shape); a[..., 0] = 0; a[..., 3] = 0; a[:, :, 5, 3] = 1
    a[:, 3, :, 4:] = 127 - rng.integers(0, 16, (N, 16, C - 4)); a[:, 3, :, 4] = 127
    for r in range(N):
        for g in range(8):
            p = x[g, :, 0, c[g, 0]]
            for j, t in ((1, W - 1), (2, 0)):
                b = rng.integers(0, 128, 16); k = int(t - np.sum(b[:14] * p[:14])) % W
                b[15] = k % 64; b[14] = (k // 64 - k % 64) % (W // 64); a[r, g, :, j] = b
    d[..., 0] = 255 * rng.integers(0, 2, (N, 8, 16)); d[..., W - 1] = 255 * rng.integers(0, 2, (N, 8, 16))
    m = rng.integers(0, 600, (8, 16, M)); u = np.where(rng.random((8, 1, M)) < 0.5, m, TOP - m)
    few = rng.integers(0, 3, (2, 16, M)) * (rng.random((2, 1, M)) < 0.5)
    d[:, 1, :, :W - 1] = 255 - (rng.random((N, 16, W - 1)) < 1.0 / C); u[1] = few[0]
    d[:, 4, :, :W - 1] = rng.integers(200, 256, (N, 16, W - 1)); u[4] = rng.integers(0, 256, (16, M))
    d[:, 6, :, :W - 1] = rng.random((N, 16, W - 1)) < 1.0 / C; u[6] = TOP - few[1]
    climb(rng, x, s, miss, u, d, a, 7)
    return pack(x, s, miss, u, d, a)
def setup_inputs_rest(rng):
    x, s, miss, u, d, a = parts(rng); d = rng.integers(1, 255, d.shape); c = newcomer(s, miss)
    kind = rng.integers(0, 4, (8, M)); kind[0] = 0; kind[1] = rng.integers(1, 3, M)
    end = np.where(rng.random((8, M)) < 0.5, 0, 15); end = np.where(end == c, 15 - end, end)
    near = (c + np.where(rng.random((8, M)) < 0.5, 1, 15)) % 16
    want = np.where(kind == 0, c, np.where(kind == 1, end, near))
    fav = np.take_along_axis(np.argsort(s, axis=1), want[:, None, :], 1)
    lab = rng.integers(0, 16, (8, 1, M)); lab[1:] = int(rng.integers(0, 16))
    s = np.take_along_axis(s, (np.arange(16)[:, None] + fav - lab) % 16, 1); miss = (miss - (fav - lab)[:, 0]) % 16
    u = np.where((kind == 3)[:, None, :], u, np.where(np.arange(16)[:, None] == lab, 0, TOP))
    return pack(x, s, miss, u, d, a)
def setup_inputs_ties(rng):
    x, s, miss, u, d, a = parts(rng)
    d = 255 * (rng.random(d.shape) < 1.0 / (N * C)).astype(np.int64); d[:, 3] = 0
    u = np.repeat(255 * rng.choice(np.array([0, 1, N * C // 2, N * C - 1]), (8, 1, M)), 16, axis=1)
    u[::2] = u[::2] + 255 * rng.integers(0, 2, u[::2].shape)
    u[3] = 255 * rng.choice(np.array([0, 1, N * C // 2, N * C]), (1, M))
    return pack(x, s, miss, u, d, a)
def setup_inputs_spread(rng):
    x, s, miss, u, d, a = parts(rng)
    d = (np.exp2(8 * rng.random((N, 8, 1, W))) * rng.random(d.shape)).astype(np.int64)
    a = np.exp2(7 * rng.random(a.shape)).astype(np.int64) * (rng.random(a.shape) > 0.0625)
    return pack(x, s, miss, rng.integers(0, 2 * N * C, u.shape), d, a)
def check_inputs(d):
    bad = []
    for k, lo, hi in (("v", 32, 200), ("sup", 0, TOP), ("dem", 0, 255), ("wt", 0, 127)):
        y = np.asarray(d[k]).astype(np.float64)
        if not np.all((y >= lo) & (y <= hi) & (y == np.floor(y))): bad.append("range of " + k)
    x = np.asarray(d["v"]).astype(np.float64).reshape(N, 8, 16, M, 16)
    if not np.all(np.abs(np.roll(x, -1, axis=4) - x) <= 3): bad.append("ring neighbours in v")
    s = np.sort(np.asarray(d["inv"]).astype(np.int64).reshape(N, 8, 16, M), axis=2)
    if not (np.all(s[:, :, 0] == -1) and np.all(s[:, :, 1] >= 0) and np.all(s[:, :, 15] <= 15) and np.all(s[:, :, 1:] > s[:, :, :-1])): bad.append("slots in inv")
    for k in ("v", "inv", "sup"):
        y = np.asarray(d[k]).astype(np.float64)
        if not np.all(y == y[:1]): bad.append(k + " is not the same on all ranks")
    return bad
def reference(v, inv, sup, dem, wt):
    x = v[0].astype(np.float32).astype(np.int64).reshape(8, 16, M, 16); n = inv[0].astype(np.int64).reshape(8, 16, M); u = sup[0].astype(np.int64).reshape(8, 16, M)
    d = dem.astype(np.float32).astype(np.int64).reshape(N, 8, 16, W); a = wt.astype(np.float32).astype(np.int64).reshape(N, 8, 16, C).transpose(0, 1, 3, 2)
    row = np.arange(16)[:, None]; slot = np.arange(16)
    def pick(k): return np.take_along_axis(x, (k & 15)[:, None, :, None], 3)[..., 0]
    c = 119 - np.add.reduce(n, axis=1)
    for step in range(RO):
        p = pick(c)
        h = np.matmul(a, p[None]) & (W - 1)
        z = np.add.reduce(np.take_along_axis(d, h.reshape(N, 8, 1, C * M), 3).reshape(N, 8, 16, C, M), axis=(0, 3)) - u
        l = np.argmax(z, axis=1)
        s = np.take_along_axis(n, l[:, None, :], 1)[:, 0]; go = s >= 0
        new = pick(s - 1) + pick(s + 1) - pick(s)
        x = np.where((slot == s[:, None, :, None]) & go[:, None, :, None], new[..., None], x)
        n = np.where((row == l[:, None, :]) & go[:, None, :], c[:, None, :], n)
        c = np.where(go, s, c)
    return {"yv": np.repeat(x.reshape(1, 128, 16 * M), N, axis=0).astype(np.float32).astype(BF), "yi": np.repeat(n.reshape(1, 128, M), N, axis=0).astype(np.float32)}

@@ -1,0 +1,470 @@
+from concourse.bass import DstId, RemoteDMATransfer
+from concourse.mybir import AluOpType as A, ActivationFunctionType as AF
+
+RO = 6
+NP = 2
+RW = 19
+BK = 32 * RW
+VSH = {(0, 0): 64, (0, 1): 20, (1, 0): 26, (1, 1): 26, (2, 0): 26, (2, 1): 26, (3, 0): 26, (3, 1): 26,
+       (4, 0): 6, (4, 1): 6, (5, 0): 6, (5, 1): 26}
+JOBS = {(3, 0): 0, (3, 1): 1, (4, 0): 2, (5, 0): 3}
+FAR = 3088
+PKW = FAR + 512
+
+SCRATCH = {"ST": ("dram", [6, 128, 512], "bfloat16"), "LD": ("dram", [6, 128, 512], "bfloat16")}
+for _d, _l in (("bfloat16", dict(TB=4096, G0=2048, G1=2048, X=8 * BK, VI=3584 + PKW, WA=64, WZ=512, ID=128, NID=128, MV=512, SW=256,
+                                 CK=128, SEL=72, CB=72, CI=8, CN=40, BS=8, SB=256, F=128, FI=16, DL=480, Y0=96, Y1=96, DF=64,
+                                 NEW=7 * 64, VL=(RO - 1) * 192, YB0=128, YB1=128, NL=256, MS=96, FL=288)),
+               ("float32", dict(IOT=128, IOM=128, IO3=8, PC=16, QM=4, HA=72, HB=72, CAP=80, D0=72, YI=256, S0=72, S1=72, AL=8,
+                                DD=8, CD=8)),
+               ("int32", dict(PI=8, SI=256, SJ=256)),
+               ("uint16", dict(OFF=7 * 16, OL=(RO - 1) * 48, HO0=128, HO1=128, OF=16))):
+    for _n in _l:
+        SCRATCH[_n] = ("sbuf", [128, _l[_n]], _d)
+for _h in (0, 1):
+    for _n in ("PA", "PB", "PK", "PS"):
+        SCRATCH["%s%d" % (_n, _h)] = ("psum", [128, 512], "float32")
+
+SEMAPHORES = (["cv", "cs", "cp", "cg", "sent", "lw", "lsi", "lvo", "lvx", "tb", "aw", "an", "out"]
+              + ["st%d" % k for k in range(NP)] + ["ad%d_%d" % (k, s) for k in range(NP) for s in range(3)]
+              + ["ax%d" % t for t in range(RO - 1)] + ["af0", "af1"])
+
+
+def lanes(topo, src, dsts):
+    far = [d for d in dsts if topo.chip(d) != topo.chip(src)]
+    near = [d for d in dsts if topo.chip(d) == topo.chip(src)]
+    res = {}
+    pool = topo.engines(src, far[0])
+    n = len(pool) // len(far)
+    for k, d in enumerate(far):
+        res[d] = pool[k * n:(k + 1) * n]
+    rest = [e for e in topo.engines(src, near[0]) if e not in pool]
+    n = len(rest) // len(near)
+    for k, d in enumerate(near):
+        res[d] = rest[k * n:(k + 1) * n]
+    return res
+
+
+def rank_program(g, core, T, topo):
+    r = T.rank_of(core)
+    if r is None:
+        return
+    cores = list(T.cores)
+    N = len(cores)
+    peers = [(r + k) % N for k in range(1, N)]
+    my = lanes(topo, core, [cores[p] for p in peers])
+    inc = {p: len(lanes(topo, cores[p], [c for c in cores if c != cores[p]])[core]) for p in peers}
+    allinc = sum(inc.values())
+    far = [s for s in range(3) if topo.chip(cores[peers[s]]) != topo.chip(core)]
+    near = [s for s in range(3) if s not in far][0]
+    order = far + [near]
+
+    Q = {"g": g, "v": g.vector, "s": g.scalar, "p": g.tensor, "y": g.sync}
+    cnt = {"g": 0, "v": 0, "s": 0, "p": 0}
+    clock = {q: {} for q in Q}
+    lastw, readers, grp, toks = {}, {}, {}, []
+    sent = ["sent", 0, {}]
+
+    def merge(a, b):
+        for k, x in b.items():
+            if a.get(k, 0) < x:
+                a[k] = x
+
+    def need(q, ts):
+        for tok in sorted(ts, key=lambda z: -z[1]):
+            if clock[q].get(tok[0], 0) < tok[1]:
+                Q[q].wait_ge(T.sem[tok[0]], tok[1])
+                merge(clock[q], tok[2])
+                clock[q][tok[0]] = tok[1]
+
+    def deps(q, rd, wr, skip=None):
+        ts = [lastw[k] for k in rd if k in lastw]
+        for k in wr:
+            ts += ([lastw[k]] if k in lastw else []) + readers.get(k, [])
+        need(q, [t for t in ts if t is not skip and not (q == "p" and t[0] == "cp")])
+
+    def note(tok, rd, wr):
+        for k in rd:
+            readers.setdefault(k, []).append(tok)
+        for k in wr:
+            lastw[k] = tok
+            readers[k] = []
+
+    def op(q, fn, rd, wr):
+        deps(q, rd, wr)
+        cnt[q] += 1
+        fn().then_inc(T.sem["c" + q], 1)
+        note(["c" + q, cnt[q], dict(clock[q])], rd, wr)
+
+    def dma(q, name, out, in_, rd, wr):
+        if name not in grp:
+            grp[name] = [name, 0, {}]
+        tok = grp[name]
+        deps(q, rd, wr, tok)
+        Q[q].dma_start(out, in_).then_inc(T.sem[name], 16)
+        tok[1] += 16
+        merge(tok[2], clock[q])
+        note(tok, rd, wr)
+
+    def fused(items, rd):
+        deps("g", rd, [])
+        tr = []
+        for s, eng, src, dst, sem in items:
+            rid, pid = topo.addr(cores[peers[s]])[:2]
+            there = (r - peers[s]) % N - 1
+            tr.append(RemoteDMATransfer(dst_ids=[DstId(rid=rid, pnc=pid)], dma_engine_mask=sum(1 << e for e in eng),
+                                        remote_sem=T.sem[sem(there)], src=src, dst=dst(there)))
+            sent[1] += len(eng)
+        g.remote_dma_fused(tr, local_sem=T.sem.sent)
+
+    def send(src, dst, sem, rd):
+        fused([(s, my[cores[peers[s]]], src, dst, lambda x: sem) for s in order], rd)
+
+    def arrive(sem, n, keys):
+        tok = [sem, n, {}]
+        toks.append(tok)
+        note(tok, [], keys)
+
+    V = g.vector
+
+    def ts(out, in0, s1, s2, o0, o1, rd, wr):
+        if o1 is None:
+            op("v", lambda: V.tensor_scalar(out, in0, s1, None, o0), rd, wr)
+        else:
+            op("v", lambda: V.tensor_scalar(out, in0, s1, s2, o0, o1), rd, wr)
+
+    def tt(out, a, b, o, rd, wr):
+        op("v", lambda: V.tensor_tensor(out, a, b, o), rd, wr)
+
+    def cp(q, out, in_, rd, wr):
+        if q == "v":
+            op(q, lambda: V.tensor_copy(out, in_), rd, wr)
+        elif q == "s":
+            op(q, lambda: g.scalar.activation(out, in_, AF.Copy), rd, wr)
+        else:
+            n = out.shape[1]
+            op(q, lambda: g.affine_select(out, in_, [[0, n]], A.is_equal, 0.0, 0, 0), rd, wr)
+
+    def ms(out, val, wr):
+        op("v", lambda: V.memset(out, val), [], wr)
+
+    def mm(out, lhsT, rhs, start, stop, rd, wr):
+        op("p", lambda: g.tensor.matmul(out, lhsT, rhs, start, stop), rd, wr)
+
+    R0 = 32 * r
+    dma("y", "lw", T.WA[:, 16 * r:16 * r + 16], T.wt[:, :], [], ["WAo"])
+    for q, s, k, c in (("s", far[0], 0, 0), ("y", far[1], 0, 0), ("s", far[0], 1, 1), ("y", far[1], 1, 1),
+                       ("s", near, 0, 1), ("y", near, 1, 1)):
+        d = 32 * peers[s] + 16 * k
+        dma(q, "st%d" % c, T.ST[2 * s + k], T.dem[d:d + 16, :], [], ["ST%d" % c])
+    dma("s", "lsi", T.SI[0:32, :], T.sup[R0:R0 + 32, :], [], ["SI"])
+    dma("y", "lsi", T.SI[32:64, :], T.sup[R0:R0 + 32, :], [], ["SI"])
+    dma("s", "lsi", T.SI[64:96, :], T.inv[R0:R0 + 32, :], [], ["SI"])
+    for h in (0, 1):
+        for t in range(4):
+            c0 = 2048 * h + 512 * t
+            dma("ys"[t % 2], "lvo", T.VI[32 * t:32 * t + 32, 512 * h:512 * h + 512], T.v[R0:R0 + 32, c0:c0 + 512], [], ["VIo"])
+    dma("y", "tb", T.TB[R0:R0 + 32, :], T.dem[R0:R0 + 32, :], ["ST1"], ["TB"])
+
+    fl = {"allow_small_or_imprecise_dtypes": True}
+    op("g", lambda: g.iota(T.PI[:, 0:1], [[0, 1]], 0, 1), [], ["PI0"])
+    op("g", lambda: g.iota(T.IOT[:, :], [[1, 128]], 0, 0, **fl), [], ["IOT"])
+    op("g", lambda: g.iota(T.IOM[:, :], [[0, 4], [1, 32]], R0, 0, **fl), [], ["IOM"])
+    op("g", lambda: g.iota(T.IO3[:, 0:6], [[1, 2], [0, 3]], 4, 0, **fl), [], ["IO3"])
+    send(T.WA[:, 16 * r:16 * r + 16], lambda s: T.WA[:, 16 * r:16 * r + 16], "aw", ["WAo"])
+    arrive("aw", allinc, ["WAx"])
+
+    def piece(s, k, eng):
+        return (s, eng, T.ST[2 * s + k], lambda x: T.LD[2 * x + k], lambda x: "ad%d_%d" % (k, x))
+
+    en = my[cores[peers[near]]]
+    fused([piece(s, 0, my[cores[peers[s]]]) for s in far], ["ST0"])
+    fused([piece(s, 1, my[cores[peers[s]]]) for s in far]
+          + [piece(near, 0, en[:len(en) // 2]), piece(near, 1, en[len(en) // 2:])], ["ST1"])
+    for q, s, k in (("s", far[0], 0), ("y", far[1], 0), ("s", near, 0), ("y", near, 1), ("s", far[0], 1), ("y", far[1], 1)):
+        key = "ad%d_%d" % (k, s)
+        arrive(key, inc[peers[s]] // (2 if s == near else 1), [key])
+        d = 32 * peers[s] + 16 * k
+        dma(q, "tb", T.TB[d:d + 16, :], T.LD[2 * s + k], [key], ["TB"])
+    for h in (0, 1):
+        for s in range(3):
+            for t in range(4):
+                c0 = 2048 * h + 512 * t
+                b0 = 1024 + 1536 * h + 512 * s
+                dma("y", "lvx", T.VI[32 * t:32 * t + 32, b0:b0 + 512], T.v[32 * peers[s]:32 * peers[s] + 32, c0:c0 + 512], ["TB"], ["VIx"])
+
+    PC = T.PC
+    ts(T.PI[:, 1:2], T.PI[:, 0:1], 4, 1, A.arith_shift_right, A.bitwise_and, ["PI0"], ["PI1"])
+    ts(T.PI[:, 2:3], T.PI[:, 0:1], 15, None, A.bitwise_and, None, ["PI0"], ["PI2"])
+    ts(T.PI[:, 3:4], T.PI[:, 0:1], 5, None, A.arith_shift_right, None, ["PI0"], ["PI3"])
+    ts(T.PI[:, 4:5], T.PI[:, 0:1], 4, None, A.arith_shift_right, None, ["PI0"], ["PI4"])
+    ms(T.CK[:, :], 532480.0, ["CK"])
+    ms(T.D0[:, :], 0.0, ["D0"])
+    ms(T.BS[:, :], 0.0, ["BS"])
+    ms(T.AL[:, :], 1.0, ["AL0", "AL1"])
+    ms(T.DL[:, :], 0.0, ["DLz"])
+    ms(T.X[:, 0:2 * BK:RW], 100.0, ["Xp"])
+    ms(T.SB[96:128, :], 1.0, ["SB3"])
+    ms(PC[0:32, 10:12], -65536.0, ["sa0"])
+    ms(PC[32:64, 10:12], -512.0, ["sa1"])
+    ms(PC[64:96, 10:11], 1.0, ["sa2"])
+    ms(PC[64:96, 11:12], 0.0, ["sa2b"])
+    cp("v", PC[:, 0:5], T.PI[:, 0:5], ["PI0", "PI1", "PI2", "PI3", "PI4"], ["PC"])
+    p_, pm, pi, qd, gr = [PC[:, k:k + 1] for k in range(5)]
+    ms(T.D0[:, 0:19:18], -67108864.0, ["D0"])
+    ms(T.BS[:, 1:6:2], 16.0 * RW, ["BS"])
+    ts(PC[:, 5:6], pm, 1000.0, p_, A.mult, A.add, ["PC"], ["ca"])
+    ts(PC[:, 6:7], pm, -1000.0, p_, A.mult, A.add, ["PC"], ["cb"])
+    ts(PC[:, 7:8], pm, 18.0, pi, A.mult, A.add, ["PC"], ["cA"])
+    ts(PC[:, 8:9], pm, 16.0, pi, A.mult, A.add, ["PC"], ["cB"])
+    ts(PC[:, 9:10], pi, float(RW), None, A.mult, None, ["PC"], ["base"])
+    ts(PC[96:128, 10:11], PC[96:128, 2:3], -32.0, 480.0, A.mult, A.add, ["PC"], ["sa3"])
+    ts(PC[96:128, 11:12], PC[96:128, 2:3], -32.0, 480.0, A.mult, A.add, ["PC"], ["sa3b"])
+    ts(PC[:, 12:13], pi, 16.0, -2.0, A.mult, A.add, ["PC"], ["pb0"])
+    ts(PC[:, 13:14], pi, 16.0, 254.0, A.mult, A.add, ["PC"], ["pb1"])
+    ms(T.D0[:, 36:53:16], -67108864.0, ["D0"])
+    ca, cb = PC[:, 5:6], PC[:, 6:7]
+    ts(T.SW[:, 0:128], T.IOM[:, :], ca, None, A.is_equal, None, ["IOM", "ca"], ["SW0"])
+    ts(T.SW[:, 128:256], T.IOM[:, :], -1000.0, cb, A.add, A.is_equal, ["IOM", "cb"], ["SW1"])
+    ts(T.CI[:, 0:6], T.IO3[:, 0:6], gr, -1.0, A.is_equal, A.mult, ["IO3", "PC"], ["CI"])
+    ts(T.QM[:, :], T.IOT[:, 0:4], qd, None, A.is_equal, None, ["IOT", "PC"], ["QM"])
+    ts(T.ID[:, :], T.IOT[:, :], p_, None, A.is_equal, None, ["IOT", "PC"], ["ID"])
+    ts(T.NID[:, :], T.IOT[:, :], p_, -1.0, A.is_equal, A.mult, ["IOT", "PC"], ["NID"])
+    ms(T.D0[:, 16:18], 1.0, ["D0"])
+    ts(T.MV[:, 0:128], T.IOT[:, :], ca, None, A.is_equal, None, ["IOT", "ca"], ["MV0"])
+    ts(T.MV[:, 128:256], T.IOT[:, :], -984.0, cb, A.add, A.is_equal, ["IOT", "cb"], ["MV1"])
+    ts(T.MV[:, 256:384], T.IOT[:, :], -16.0, ca, A.add, A.is_equal, ["IOT", "ca"], ["MV2"])
+    ts(T.MV[:, 384:512], T.IOT[:, :], -1000.0, cb, A.add, A.is_equal, ["IOT", "cb"], ["MV3"])
+    ms(T.D0[:, 34:36], 1.0, ["D0"])
+    ts(T.HA[:, :], T.IOT[:, 0:72], PC[:, 7:8], None, A.is_equal, None, ["IOT", "cA"], ["HA"])
+    ts(T.HB[:, :], T.IOT[:, 0:72], -36.0, PC[:, 8:9], A.add, A.is_equal, ["IOT", "cB"], ["HB"])
+    ts(T.CN[:, 0:34], T.HA[:, 0:34], T.QM[:, 2:3], None, A.mult, None, ["HA", "QM"], ["CN"])
+    tt(T.S0[:, :], T.HA[:, :], T.HB[:, :], A.add, ["HA", "HB"], ["S0"])
+    sas = ["sa0", "sa1", "sa2", "sa2b", "sa3", "sa3b"]
+    ts(T.HA[:, :], T.HA[:, :], PC[:, 10:11], None, A.mult, None, ["HA"] + sas, ["HA"])
+    ts(T.HB[:, :], T.HB[:, :], PC[:, 11:12], None, A.mult, None, ["HB"] + sas, ["HB"])
+    ts(T.SEL[:, :], T.S0[:, :], 512.0, None, A.mult, None, ["S0"], ["SEL"])
+    tt(T.CB[:, :], T.HA[:, :], T.HB[:, :], A.add, ["HA", "HB"], ["CB"])
+    ts(T.SJ[0:32, :], T.SI[0:32, :], 7, None, A.arith_shift_right, None, ["SI"], ["SJ0"])
+    ts(T.SJ[32:64, :], T.SI[32:64, :], 127, None, A.bitwise_and, None, ["SI"], ["SJ1"])
+    ms(T.CB[96:128, 16:18], -1048576.0, ["CB"])
+    ts(T.SB[64:96, :], T.SI[64:96, :], 1.0, None, A.add, None, ["SI"], ["SB2"])
+    ms(T.CB[96:128, 34:36], -1048576.0, ["CB"])
+    cp("v", T.SB[0:64, :], T.SJ[0:64, :], ["SJ0", "SJ1"], ["SB0"])
+    SBK = ["SB0", "SB2", "SB3"]
+    for h in (0, 1):
+        mm(T["PS%d" % h][:, 8:14], T.SB[:, 128 * h:128 * h + 128], T.CI[:, 0:6], True, True, SBK + ["CI"], ["PS%d" % h])
+        mm(T["PS%d" % h][:, 16:50], T.SB[:, 128 * h:128 * h + 128], T.CN[:, 0:34], True, True, SBK + ["CN"], ["PS%d" % h])
+    for k in range(16):
+        cp("v", T.X[:, k + 2:2 * BK:RW], T.VI[:, k:1024:16], ["VIo"], ["Xi%d" % k])
+    cp("v", T.X[:, 1:2 * BK:RW], T.VI[:, 15:1024:16], ["VIo"], ["Xi16"])
+    cp("v", T.X[:, 18:2 * BK:RW], T.VI[:, 0:1024:16], ["VIo"], ["Xi17"])
+    XI = ["Xp"] + ["Xi%d" % k for k in range(18)]
+    for h in (0, 1):
+        ts(T.FI[:, 8 * h:8 * h + 6], T["PS%d" % h][:, 8:14], 137.0, None, A.add, None, ["PS%d" % h], ["FI%d" % h])
+        ts(T.F[:, 8 * h:8 * h + 6], T["PS%d" % h][:, 8:14], 136.0, None, A.add, None, ["PS%d" % h], ["F0_%d" % h])
+        ts(T.CAP[:, 40 * h:40 * h + 34], T["PS%d" % h][:, 16:50], 0.0, 100.0, A.is_gt, A.mult, ["PS%d" % h], ["CAP%d" % h])
+
+    def new(t, h):
+        return T.MS[:, 48 * h:48 * h + 32] if t == RO - 1 else T.NEW[:, 64 * t + 32 * h:64 * t + 32 * h + 32]
+
+    def pick(t, h, Fap, fk):
+        PS, Y, hs = T["PS%d" % h], T["Y%d" % h], str(h)
+        for b in (0, 1):
+            for m in (0, 1):
+                mm(PS[:, b:6:2], T.MV[:, 128 * (2 * m + b):128 * (2 * m + b) + 128], Fap[:, 3 * m:3 * m + 3], False,
+                   b == 1 and m == 1, ["MV%d" % (2 * m + b), fk + "_%d" % m if t < RO else fk], ["PS" + hs])
+        if t < RO:
+            f0 = 8 * (2 * t + h)
+            tt(T.DD[:, 4 * h:4 * h + 2], T.F[:, f0:f0 + 6:3], Fap[:, 0:6:3], A.subtract,
+               [fk + "_0", fk + "_1"] + (["F0_" + hs] if t == 0 else []), ["DD" + hs])
+        o0 = 16 * t + 6 * h
+        ok = "OFF%d_%d" % (t, h)
+        ts(T.OFF[:, o0:o0 + 6], PS[:, 0:6], PC[:, 9:10], None, A.add, None, ["PS" + hs, "base"], [ok])
+        fin = t == RO - 1
+        c0 = 4 * h
+        if fin:
+            tt(T.CD[:, c0:c0 + 2], PS[:, 2:4], T.BS[:, 2:4], A.subtract, ["PS" + hs, "BS"], ["CD" + hs])
+        cp("v", Y[:, :], T.X[:, BK * h:BK * h + BK].indirect(T.OFF[:, o0:o0 + 6]), [ok, "X" + hs, "Xl" + hs, "Xr" + hs] + XI, ["Y" + hs])
+        if fin:
+            ts(T.CD[:, c0 + 2:c0 + 4], T.CD[:, c0:c0 + 2], 1.0, float(FAR), A.is_le, A.mult, ["CD" + hs], ["CE" + hs])
+        tt(T.DF[:, 32 * h:32 * h + 32], Y[:, 0:32], Y[:, 32:64], A.subtract, ["Y" + hs], ["DF" + hs])
+        if fin:
+            tt(T.MS[:, 48 * h + 32:48 * h + 34], T.CD[:, c0:c0 + 2], T.CD[:, c0 + 2:c0 + 4], A.add, ["CD" + hs, "CE" + hs], ["MC" + hs])
+        tt(new(t, h), T.DF[:, 32 * h:32 * h + 32], Y[:, 64:96], A.add, ["Y" + hs, "DF" + hs], ["NEW%d_%d" % (t, h)])
+
+    def opens(h, places):
+        hs = str(h)
+        mm(T["PS" + hs][:, 0:6], T.ID[:, :], T.BS[:, 0:6], True, False, ["ID", "BS"], ["PS" + hs])
+        if places:
+            mm(T["PB" + hs][:, 0:128], T.ID[:, :], T.CK[:, :], True, False, ["ID", "CK"], ["PB" + hs])
+
+    def places1(t, h):
+        hs, n0 = str(h), 64 * t + 32 * h
+        for n in ("PA", "PB"):
+            for q in range(4):
+                mm(T[n + hs][:, 32 * q:32 * q + 32], T.WZ[:, 128 * q:128 * q + 128], T.NEW[:, n0:n0 + 32], n == "PA", n == "PA",
+                   ["WZ%d" % q, "NEW%d_%d" % (t, h)], [n + hs])
+
+    def places2(h):
+        hs = str(h)
+        ts(T["YB" + hs][:, :], T["PA" + hs][:, 0:128], 530432.5, None, A.add, None, ["PA" + hs], ["YB" + hs])
+        mm(T["PB" + hs][:, 0:128], T.NID[:, :], T["YB" + hs][:, :], False, True, ["NID", "YB" + hs], ["PB" + hs])
+
+    def places3(h):
+        hs = str(h)
+        cp("v", T["HO" + hs][:, :], T["PB" + hs][:, 0:128], ["PB" + hs], ["HO" + hs])
+
+    def keybase(t, h):
+        hs = str(h)
+        mm(T["PK" + hs][:, 0:68], T.SB[:, 128 * h:128 * h + 128], T.CB[:, 0:68], True, False, SBK + ["CB"], ["PK" + hs])
+        for u in range(t):
+            d0 = 40 * (2 * u + h)
+            mm(T["PK" + hs][:, 0:34], T.ID[:, :], T.DL[:, d0:d0 + 34], False, False,
+               ["ID", "DLz", "DL%d_%d_0" % (u, h), "DL%d_%d_1" % (u, h)], ["PK" + hs])
+
+    def gather(q, t, h):
+        hs = str(h)
+        c = 128 - VSH.get((t, h), 0)
+        a, b = (0, c) if q == "s" else (c, 128)
+        if a < b:
+            cp(q, T["G" + hs][:, 16 * a:16 * b], T.TB[:, :].indirect(T["HO" + hs][:, a:b]), ["TB", "HO" + hs], ["G" + q + hs])
+
+    def update(t, h):
+        hs, o0 = str(h), 16 * t + 6 * h + 2
+        cp("v", T.X[:, BK * h:BK * h + BK].indirect(T.OFF[:, o0:o0 + 2]), new(t, h),
+           ["OFF%d_%d" % (t, h), "NEW%d_%d" % (t, h)], ["X" + hs, "Xl" + hs, "Xr" + hs])
+
+    def labels(t, h):
+        hs, d0 = str(h), 40 * (2 * t + h)
+        for m in (0, 1):
+            ts(T.DL[:, d0 + 18 * m:d0 + 18 * m + 16], T["PK" + hs][:, 18 * m:18 * m + 16], T["S" + hs][:, 18 * m + 15:18 * m + 16],
+               T.DD[:, 4 * h + m:4 * h + m + 1], A.is_equal, A.mult, ["PK" + hs, "S" + hs, "DD" + hs, "DLz"], ["DL%d_%d_%d" % (t, h, m)])
+
+    def apply(t, h):
+        for s in range(3):
+            x0, o0, n0 = BK * (2 + 3 * h + s), 48 * t + 16 * s + 6 * h + 2, 192 * t + 64 * s + 32 * h
+            cp("v", T.X[:, x0:x0 + BK].indirect(T.OL[:, o0:o0 + 2]), T.VL[:, n0:n0 + 32],
+               ["L%d_%d" % (t, h)] + ["Xe%d" % k for k in range(16)], ["Xx%d_%d" % (h, s)])
+
+    def pack(own, ks, q):
+        x0, x1, v0, v1 = (0, 2 * BK, 0, 1024) if own else (2 * BK, 8 * BK, 1024, 4096)
+        rd = ["X0", "X1"] if own else ["Xx%d_%d" % (h, s) for h in (0, 1) for s in range(3)]
+        for k in ks:
+            cp(q, T.VI[:, v0 + k:v1:16], T.X[:, x0 + k + 2:x1:RW], rd, ["O%d_%d" % (own, k)])
+
+    def store(h, s, qs, rd):
+        d = R0 if s is None else 32 * peers[s]
+        v0 = 512 * h if s is None else 1024 + 1536 * h + 512 * s
+        for t in range(4):
+            c0 = 2048 * h + 512 * t
+            dma(qs[t % len(qs)], "out", T.yv[d:d + 32, c0:c0 + 512], T.VI[32 * t:32 * t + 32, v0:v0 + 512], rd, [])
+
+    def finish(h, qs):
+        hs = str(h)
+        for b in (0, 1):
+            f0 = 144 * h + 32 + b
+            ts(T.OF[:, 8 * h + b:8 * h + 6:2], T.FL[:, f0:144 * h + 144:48], PC[:, 12 + b:13 + b], None, A.add, None,
+               ["LF" + hs, "pb%d" % b], ["OF%d_%d" % (h, b)])
+        for s in range(3):
+            v0, f0 = 1024 + 1536 * h + 512 * s, 144 * h + 48 * s
+            cp("v", T.VI[:, v0:v0 + PKW].indirect(T.OF[:, 8 * h + 2 * s:8 * h + 2 * s + 2]), T.FL[:, f0:f0 + 32],
+               ["LF" + hs, "OF%d_0" % h, "OF%d_1" % h] + ["O0_%d" % k for k in range(16)], ["VIw", "B%d_%d" % (h, s)])
+            store(h, s, qs, ["B%d_%d" % (h, s)])
+
+    for h in (0, 1):
+        opens(h, True)
+        pick(RO, h, T.FI[:, 8 * h:8 * h + 6], "FI%d" % h)
+    for x in range(N):
+        for m in (0, 1):
+            mm(T.PK0[:, 32 * x + 16 * m:32 * x + 16 * m + 16], T.SW[:, 128 * m:128 * m + 128], T.WA[:, 16 * x:16 * x + 16],
+               True, True, ["SW%d" % m, "WAo", "WAx"], ["PK0"])
+    for q in range(4):
+        ts(T.WZ[:, 128 * q:128 * q + 128], T.PK0[:, 0:128], T.QM[:, q:q + 1], None, A.mult, None, ["PK0", "QM"], ["WZ%d" % q])
+    for h in (0, 1):
+        places1(RO, h)
+    for h in (0, 1):
+        places2(h)
+    for h in (0, 1):
+        places3(h)
+        keybase(0, h)
+        opens(h, True)
+    for h in (0, 1):
+        gather("v", 0, h)
+        gather("s", 0, h)
+
+    spread = {(0, 1): range(0, 4), (1, 0): range(4, 8), (1, 1): range(8, 12), (2, 0): range(12, 16)}
+    for t in range(RO):
+        last = t == RO - 1
+        for h in (0, 1):
+            hs = str(h)
+            PK, S, G = T["PK" + hs], T["S" + hs], T["G" + hs]
+            for e in range(16):
+                mm(PK[:, 0:68], G[:, e:2048:16], T.SEL[:, 0:68], False, e == 15, ["Gs" + hs, "Gv" + hs, "SEL"], ["PK" + hs])
+            op("v", lambda: V.tensor_tensor_scan(S[:, 0:68], T.D0[:, 0:68], PK[:, 0:68], 0.0, A.add, A.max), ["D0", "PK" + hs], ["S" + hs])
+            f0 = 8 * (2 * t + 2 + h)
+            fk = "F%d_%d" % (t + 1, h)
+            for m in (0, 1):
+                ts(T.F[:, f0 + 3 * m:f0 + 3 * m + 3], S[:, 18 * m + 15:18 * m + 18], S[:, 51 + 16 * m:52 + 16 * m],
+                   T.AL[:, 4 * h + m:4 * h + m + 1], A.subtract, A.mult, ["S" + hs, "AL" + hs], [fk + "_%d" % m])
+            pick(t, h, T.F[:, f0:f0 + 6], fk)
+            if not last:
+                places1(t, h)
+                update(t, h)
+                places2(h)
+                labels(t, h)
+                places3(h)
+                keybase(t + 1, h)
+                opens(h, t + 2 < RO)
+                gather("s", t + 1, h)
+                ts(T.AL[:, 4 * h:4 * h + 2], T.F[:, f0:f0 + 6:3], 0.0, None, A.is_gt, None, [fk + "_0", fk + "_1"], ["AL" + hs])
+                gather("v", t + 1, h)
+                x0 = BK * h
+                cp("g", T.X[:, x0 + 1:x0 + BK:RW], T.X[:, x0 + 17:x0 + BK:RW], ["X" + hs], ["Xl" + hs])
+                cp("g", T.X[:, x0 + 18:x0 + BK:RW], T.X[:, x0 + 2:x0 + BK:RW], ["X" + hs], ["Xr" + hs])
+                if h == 1:
+                    send(T.OFF[:, 16 * t:16 * t + 12], lambda s: T.OL[:, 48 * t + 16 * s:48 * t + 16 * s + 12],
+                         "ax%d" % t, ["OFF%d_0" % t, "OFF%d_1" % t])
+                    send(T.NEW[:, 64 * t:64 * t + 64], lambda s: T.VL[:, 192 * t + 64 * s:192 * t + 64 * s + 64],
+                         "ax%d" % t, ["NEW%d_0" % t, "NEW%d_1" % t])
+                    arrive("ax%d" % t, 2 * allinc, ["L%d_0" % t, "L%d_1" % t])
+                for k in spread.get((t, h), []):
+                    cp("g", T.X[:, 2 * BK + k + 2:8 * BK:RW], T.VI[:, 1024 + k:4096:16], ["VIx"], ["Xe%d" % k])
+            else:
+                send(T.MS[:, 48 * h:48 * h + 34], lambda s: T.FL[:, 144 * h + 48 * s:144 * h + 48 * s + 34],
+                     "af" + hs, ["NEW%d_%d" % (t, h), "MC" + hs])
+                arrive("af" + hs, allinc, ["LF" + hs])
+                mm(T["PA" + hs][:, 0:34], T.SB[:, 128 * h:128 * h + 128], T.CN[:, 0:34], True, False, SBK + ["CN"], ["PA" + hs])
+                update(t, h)
+                labels(t, h)
+                for u in range(RO):
+                    d0 = 40 * (2 * u + h)
+                    mm(T["PA" + hs][:, 0:34], T.ID[:, :], T.DL[:, d0:d0 + 34], False, u == RO - 1,
+                       ["ID", "DL%d_%d_0" % (u, h), "DL%d_%d_1" % (u, h)], ["PA" + hs])
+                for m in (0, 1):
+                    c0, k0 = 64 * r + 32 * m + h, 40 * h + 18 * m
+                    tt(T.NL[:, c0:c0 + 31:2], T["PA" + hs][:, 18 * m:18 * m + 16], T.CAP[:, k0:k0 + 16], A.min,
+                       ["PA" + hs, "CAP" + hs], ["NL%d_%d" % (h, m)])
+            if (t, h) in JOBS:
+                apply(JOBS[(t, h)], 0)
+                apply(JOBS[(t, h)], 1)
+
+    NLK = ["NL0_0", "NL0_1", "NL1_0", "NL1_1"]
+    send(T.NL[:, 64 * r:64 * r + 64], lambda s: T.NL[:, 64 * r:64 * r + 64], "an", NLK)
+    arrive("an", allinc, ["NLx"])
+    pack(1, range(16), "s")
+    OWN = ["O1_%d" % k for k in range(16)]
+    store(0, None, "y", OWN)
+    store(1, None, "y", OWN)
+    apply(RO - 2, 0)
+    apply(RO - 2, 1)
+    pack(0, range(0, 2), "g")
+    pack(0, range(2, 6), "s")
+    pack(0, range(6, 16), "v")
+    finish(0, "ys")
+    finish(1, "ys")
+    for h in (0, 1):
+        mm(T["PB%d" % h][:, 0:128], T.NL[:, h:256:2], T.ID[:, :], True, True, NLK + ["NLx", "ID"], ["PB%d" % h])
+        ts(T.YI[:, 128 * h:128 * h + 128], T["PB%d" % h][:, 0:128], -1.0, None, A.add, None, ["PB%d" % h], ["YI%d" % h])
+    dma("y", "out", T.yi[:, :], T.YI[:, :], ["YI0", "YI1"], [])
+    need("g", [["c" + q, cnt[q], {}] for q in cnt] + list(grp.values()) + toks + [sent])

@@ -5,19 +5,19 @@ RO = 6
 NP = 2
 RW = 19
 BK = 32 * RW
-VSH = {(0, 0): 64, (0, 1): 20, (1, 0): 26, (1, 1): 26, (2, 0): 26, (2, 1): 26, (3, 0): 26, (3, 1): 26,
-       (4, 0): 6, (4, 1): 6, (5, 0): 6, (5, 1): 26}
+VSH = {(0, 0): 64, (0, 1): 24, (1, 0): 30, (1, 1): 30, (2, 0): 30, (2, 1): 30, (3, 0): 30, (3, 1): 30,
+       (4, 0): 8, (4, 1): 8, (5, 0): 8, (5, 1): 30}
 JOBS = {(3, 0): 0, (3, 1): 1, (4, 0): 2, (5, 0): 3}
 FAR = 3088
 PKW = FAR + 512
 
 SCRATCH = {"ST": ("dram", [6, 128, 512], "bfloat16"), "LD": ("dram", [6, 128, 512], "bfloat16")}
-for _d, _l in (("bfloat16", dict(TB=4096, G0=2048, G1=2048, X=8 * BK, VI=3584 + PKW, WA=64, WZ=512, ID=128, NID=128, MV=512, SW=256,
+for _d, _l in (("bfloat16", dict(TB=4096, G0=2048, G1=2048, X=8 * BK, VI=3584 + PKW, WA=64, WZ=512, ID=128, MV=512, SW=256,
                                  CK=128, SEL=72, CB=72, CI=8, CN=40, BS=8, SB=256, F=128, FI=16, DL=480, Y0=96, Y1=96, DF=64,
-                                 NEW=7 * 64, VL=(RO - 1) * 192, YB0=128, YB1=128, NL=256, MS=96, FL=288)),
+                                 NEW=6 * 64, VL=(RO - 1) * 192, NL=256, MS=96, FL=288)),
                ("float32", dict(IOT=128, IOM=128, IO3=8, PC=16, QM=4, HA=72, HB=72, CAP=80, D0=72, YI=256, S0=72, S1=72, AL=8,
                                 DD=8, CD=8)),
-               ("int32", dict(PI=8, SI=256, SJ=256)),
+               ("int32", dict(PI=8, SI=256, SJ=256, HI0=128, HI1=128, HJ0=128, HJ1=128)),
                ("uint16", dict(OFF=7 * 16, OL=(RO - 1) * 48, HO0=128, HO1=128, OF=16))):
     for _n in _l:
         SCRATCH[_n] = ("sbuf", [128, _l[_n]], _d)
@@ -198,7 +198,7 @@ def rank_program(g, core, T, topo):
     ts(T.PI[:, 2:3], T.PI[:, 0:1], 15, None, A.bitwise_and, None, ["PI0"], ["PI2"])
     ts(T.PI[:, 3:4], T.PI[:, 0:1], 5, None, A.arith_shift_right, None, ["PI0"], ["PI3"])
     ts(T.PI[:, 4:5], T.PI[:, 0:1], 4, None, A.arith_shift_right, None, ["PI0"], ["PI4"])
-    ms(T.CK[:, :], 532480.0, ["CK"])
+    ms(T.CK[:, :], 0.0, ["CK"])
     ms(T.D0[:, :], 0.0, ["D0"])
     ms(T.BS[:, :], 0.0, ["BS"])
     ms(T.AL[:, :], 1.0, ["AL0", "AL1"])
@@ -229,7 +229,6 @@ def rank_program(g, core, T, topo):
     ts(T.CI[:, 0:6], T.IO3[:, 0:6], gr, -1.0, A.is_equal, A.mult, ["IO3", "PC"], ["CI"])
     ts(T.QM[:, :], T.IOT[:, 0:4], qd, None, A.is_equal, None, ["IOT", "PC"], ["QM"])
     ts(T.ID[:, :], T.IOT[:, :], p_, None, A.is_equal, None, ["IOT", "PC"], ["ID"])
-    ts(T.NID[:, :], T.IOT[:, :], p_, -1.0, A.is_equal, A.mult, ["IOT", "PC"], ["NID"])
     ms(T.D0[:, 16:18], 1.0, ["D0"])
     ts(T.MV[:, 0:128], T.IOT[:, :], ca, None, A.is_equal, None, ["IOT", "ca"], ["MV0"])
     ts(T.MV[:, 128:256], T.IOT[:, :], -984.0, cb, A.add, A.is_equal, ["IOT", "cb"], ["MV1"])
@@ -270,14 +269,16 @@ def rank_program(g, core, T, topo):
 
     def pick(t, h, Fap, fk):
         PS, Y, hs = T["PS%d" % h], T["Y%d" % h], str(h)
-        for b in (0, 1):
-            for m in (0, 1):
+        for m in (0, 1):
+            for b in (0, 1):
                 mm(PS[:, b:6:2], T.MV[:, 128 * (2 * m + b):128 * (2 * m + b) + 128], Fap[:, 3 * m:3 * m + 3], False,
                    b == 1 and m == 1, ["MV%d" % (2 * m + b), fk + "_%d" % m if t < RO else fk], ["PS" + hs])
         if t < RO:
             f0 = 8 * (2 * t + h)
             tt(T.DD[:, 4 * h:4 * h + 2], T.F[:, f0:f0 + 6:3], Fap[:, 0:6:3], A.subtract,
                [fk + "_0", fk + "_1"] + (["F0_" + hs] if t == 0 else []), ["DD" + hs])
+            if t < RO - 1:
+                ts(T.AL[:, 4 * h:4 * h + 2], Fap[:, 0:6:3], 0.0, None, A.is_gt, None, [fk + "_0", fk + "_1"], ["AL" + hs])
         o0 = 16 * t + 6 * h
         ok = "OFF%d_%d" % (t, h)
         ts(T.OFF[:, o0:o0 + 6], PS[:, 0:6], PC[:, 9:10], None, A.add, None, ["PS" + hs, "base"], [ok])
@@ -291,29 +292,29 @@ def rank_program(g, core, T, topo):
         tt(T.DF[:, 32 * h:32 * h + 32], Y[:, 0:32], Y[:, 32:64], A.subtract, ["Y" + hs], ["DF" + hs])
         if fin:
             tt(T.MS[:, 48 * h + 32:48 * h + 34], T.CD[:, c0:c0 + 2], T.CD[:, c0 + 2:c0 + 4], A.add, ["CD" + hs, "CE" + hs], ["MC" + hs])
-        tt(new(t, h), T.DF[:, 32 * h:32 * h + 32], Y[:, 64:96], A.add, ["Y" + hs, "DF" + hs], ["NEW%d_%d" % (t, h)])
+        if t < RO:
+            tt(new(t, h), T.DF[:, 32 * h:32 * h + 32], Y[:, 64:96], A.add, ["Y" + hs, "DF" + hs], ["NEW%d_%d" % (t, h)])
 
     def opens(h, places):
         hs = str(h)
         mm(T["PS" + hs][:, 0:6], T.ID[:, :], T.BS[:, 0:6], True, False, ["ID", "BS"], ["PS" + hs])
         if places:
-            mm(T["PB" + hs][:, 0:128], T.ID[:, :], T.CK[:, :], True, False, ["ID", "CK"], ["PB" + hs])
+            mm(T["PA" + hs][:, 0:128], T.ID[:, :], T.CK[:, :], True, False, ["ID", "CK"], ["PA" + hs])
 
-    def places1(t, h):
-        hs, n0 = str(h), 64 * t + 32 * h
-        for n in ("PA", "PB"):
+    def places1(h):
+        hs = str(h)
+        for x, k in ((T["Y" + hs][:, 64:96], "Y"), (T.DF[:, 32 * h:32 * h + 32], "DF")):
             for q in range(4):
-                mm(T[n + hs][:, 32 * q:32 * q + 32], T.WZ[:, 128 * q:128 * q + 128], T.NEW[:, n0:n0 + 32], n == "PA", n == "PA",
-                   ["WZ%d" % q, "NEW%d_%d" % (t, h)], [n + hs])
+                mm(T["PA" + hs][:, 32 * q:32 * q + 32], T.WZ[:, 128 * q:128 * q + 128], x, False, k == "DF" and q == 3,
+                   ["WZ%d" % q, k + hs], ["PA" + hs])
 
-    def places2(h):
+    def places2(h, between):
         hs = str(h)
-        ts(T["YB" + hs][:, :], T["PA" + hs][:, 0:128], 530432.5, None, A.add, None, ["PA" + hs], ["YB" + hs])
-        mm(T["PB" + hs][:, 0:128], T.NID[:, :], T["YB" + hs][:, :], False, True, ["NID", "YB" + hs], ["PB" + hs])
-
-    def places3(h):
-        hs = str(h)
-        cp("v", T["HO" + hs][:, :], T["PB" + hs][:, 0:128], ["PB" + hs], ["HO" + hs])
+        cp("v", T["HI" + hs][:, :], T["PA" + hs][:, 0:128], ["PA" + hs], ["HI" + hs])
+        between(0)
+        ts(T["HJ" + hs][:, :], T["HI" + hs][:, :], 4095, None, A.bitwise_and, None, ["HI" + hs], ["HJ" + hs])
+        between(1)
+        cp("v", T["HO" + hs][:, :], T["HJ" + hs][:, :], ["HJ" + hs], ["HO" + hs])
 
     def keybase(t, h):
         hs = str(h)
@@ -335,11 +336,10 @@ def rank_program(g, core, T, topo):
         cp("v", T.X[:, BK * h:BK * h + BK].indirect(T.OFF[:, o0:o0 + 2]), new(t, h),
            ["OFF%d_%d" % (t, h), "NEW%d_%d" % (t, h)], ["X" + hs, "Xl" + hs, "Xr" + hs])
 
-    def labels(t, h):
+    def labels(t, h, m):
         hs, d0 = str(h), 40 * (2 * t + h)
-        for m in (0, 1):
-            ts(T.DL[:, d0 + 18 * m:d0 + 18 * m + 16], T["PK" + hs][:, 18 * m:18 * m + 16], T["S" + hs][:, 18 * m + 15:18 * m + 16],
-               T.DD[:, 4 * h + m:4 * h + m + 1], A.is_equal, A.mult, ["PK" + hs, "S" + hs, "DD" + hs, "DLz"], ["DL%d_%d_%d" % (t, h, m)])
+        ts(T.DL[:, d0 + 18 * m:d0 + 18 * m + 16], T["PK" + hs][:, 18 * m:18 * m + 16], T["S" + hs][:, 18 * m + 15:18 * m + 16],
+           T.DD[:, 4 * h + m:4 * h + m + 1], A.is_equal, A.mult, ["PK" + hs, "S" + hs, "DD" + hs, "DLz"], ["DL%d_%d_%d" % (t, h, m)])
 
     def apply(t, h):
         for s in range(3):
@@ -382,17 +382,16 @@ def rank_program(g, core, T, topo):
     for q in range(4):
         ts(T.WZ[:, 128 * q:128 * q + 128], T.PK0[:, 0:128], T.QM[:, q:q + 1], None, A.mult, None, ["PK0", "QM"], ["WZ%d" % q])
     for h in (0, 1):
-        places1(RO, h)
+        places1(h)
     for h in (0, 1):
-        places2(h)
-    for h in (0, 1):
-        places3(h)
+        places2(h, lambda k: None)
         keybase(0, h)
         opens(h, True)
     for h in (0, 1):
         gather("v", 0, h)
         gather("s", 0, h)
 
+    later = []
     spread = {(0, 1): range(0, 4), (1, 0): range(4, 8), (1, 1): range(8, 12), (2, 0): range(12, 16)}
     for t in range(RO):
         last = t == RO - 1
@@ -401,6 +400,10 @@ def rank_program(g, core, T, topo):
             PK, S, G = T["PK" + hs], T["S" + hs], T["G" + hs]
             for e in range(16):
                 mm(PK[:, 0:68], G[:, e:2048:16], T.SEL[:, 0:68], False, e == 15, ["Gs" + hs, "Gv" + hs, "SEL"], ["PK" + hs])
+            while later:
+                u, x = later.pop()
+                keybase(u + 1, x)
+                opens(x, u + 2 < RO)
             op("v", lambda: V.tensor_tensor_scan(S[:, 0:68], T.D0[:, 0:68], PK[:, 0:68], 0.0, A.add, A.max), ["D0", "PK" + hs], ["S" + hs])
             f0 = 8 * (2 * t + 2 + h)
             fk = "F%d_%d" % (t + 1, h)
@@ -409,15 +412,11 @@ def rank_program(g, core, T, topo):
                    T.AL[:, 4 * h + m:4 * h + m + 1], A.subtract, A.mult, ["S" + hs, "AL" + hs], [fk + "_%d" % m])
             pick(t, h, T.F[:, f0:f0 + 6], fk)
             if not last:
-                places1(t, h)
-                update(t, h)
-                places2(h)
-                labels(t, h)
-                places3(h)
-                keybase(t + 1, h)
-                opens(h, t + 2 < RO)
+                places1(h)
+                places2(h, lambda m: labels(t, h, m))
+                later.append((t, h))
                 gather("s", t + 1, h)
-                ts(T.AL[:, 4 * h:4 * h + 2], T.F[:, f0:f0 + 6:3], 0.0, None, A.is_gt, None, [fk + "_0", fk + "_1"], ["AL" + hs])
+                update(t, h)
                 gather("v", t + 1, h)
                 x0 = BK * h
                 cp("g", T.X[:, x0 + 1:x0 + BK:RW], T.X[:, x0 + 17:x0 + BK:RW], ["X" + hs], ["Xl" + hs])
@@ -436,7 +435,8 @@ def rank_program(g, core, T, topo):
                 arrive("af" + hs, allinc, ["LF" + hs])
                 mm(T["PA" + hs][:, 0:34], T.SB[:, 128 * h:128 * h + 128], T.CN[:, 0:34], True, False, SBK + ["CN"], ["PA" + hs])
                 update(t, h)
-                labels(t, h)
+                labels(t, h, 0)
+                labels(t, h, 1)
                 for u in range(RO):
                     d0 = 40 * (2 * u + h)
                     mm(T["PA" + hs][:, 0:34], T.ID[:, :], T.DL[:, d0:d0 + 34], False, u == RO - 1,

@@ -5,8 +5,8 @@ RO = 6
 NP = 2
 RW = 19
 BK = 32 * RW
-VSH = {(0, 0): 64, (0, 1): 24, (1, 0): 30, (1, 1): 30, (2, 0): 30, (2, 1): 30, (3, 0): 30, (3, 1): 30,
-       (4, 0): 8, (4, 1): 8, (5, 0): 8, (5, 1): 30}
+VSH = {(t, h): (16, 8) for t in range(RO) for h in (0, 1)}
+VSH.update({(0, 0): (64, 0), (0, 1): (24, 0), (4, 0): (6, 0), (4, 1): (6, 0), (5, 0): (6, 0)})
 JOBS = {(3, 0): 0, (3, 1): 1, (4, 0): 2, (5, 0): 3}
 FAR = 3088
 PKW = FAR + 512
@@ -264,6 +264,8 @@ def rank_program(g, core, T, topo):
         ts(T.F[:, 8 * h:8 * h + 6], T["PS%d" % h][:, 8:14], 136.0, None, A.add, None, ["PS%d" % h], ["F0_%d" % h])
         ts(T.CAP[:, 40 * h:40 * h + 34], T["PS%d" % h][:, 16:50], 0.0, 100.0, A.is_gt, A.mult, ["PS%d" % h], ["CAP%d" % h])
 
+    later, fill = [], []
+
     def new(t, h):
         return T.MS[:, 48 * h:48 * h + 32] if t == RO - 1 else T.NEW[:, 64 * t + 32 * h:64 * t + 32 * h + 32]
 
@@ -273,12 +275,18 @@ def rank_program(g, core, T, topo):
             for b in (0, 1):
                 mm(PS[:, b:6:2], T.MV[:, 128 * (2 * m + b):128 * (2 * m + b) + 128], Fap[:, 3 * m:3 * m + 3], False,
                    b == 1 and m == 1, ["MV%d" % (2 * m + b), fk + "_%d" % m if t < RO else fk], ["PS" + hs])
+        while later:
+            u, x = later.pop()
+            keybase(u + 1, x)
+            opens(x, u + 2 < RO)
         if t < RO:
             f0 = 8 * (2 * t + h)
             tt(T.DD[:, 4 * h:4 * h + 2], T.F[:, f0:f0 + 6:3], Fap[:, 0:6:3], A.subtract,
                [fk + "_0", fk + "_1"] + (["F0_" + hs] if t == 0 else []), ["DD" + hs])
             if t < RO - 1:
                 ts(T.AL[:, 4 * h:4 * h + 2], Fap[:, 0:6:3], 0.0, None, A.is_gt, None, [fk + "_0", fk + "_1"], ["AL" + hs])
+            while fill:
+                fill.pop(0)()
         o0 = 16 * t + 6 * h
         ok = "OFF%d_%d" % (t, h)
         ts(T.OFF[:, o0:o0 + 6], PS[:, 0:6], PC[:, 9:10], None, A.add, None, ["PS" + hs, "base"], [ok])
@@ -324,12 +332,13 @@ def rank_program(g, core, T, topo):
             mm(T["PK" + hs][:, 0:34], T.ID[:, :], T.DL[:, d0:d0 + 34], False, False,
                ["ID", "DLz", "DL%d_%d_0" % (u, h), "DL%d_%d_1" % (u, h)], ["PK" + hs])
 
-    def gather(q, t, h):
+    def gather(q, t, h, part=0):
         hs = str(h)
-        c = 128 - VSH.get((t, h), 0)
-        a, b = (0, c) if q == "s" else (c, 128)
+        w = VSH[(t, h)]
+        a = 128 - sum(w[part:])
+        a, b = (0, a) if q == "s" else (a, a + w[part])
         if a < b:
-            cp(q, T["G" + hs][:, 16 * a:16 * b], T.TB[:, :].indirect(T["HO" + hs][:, a:b]), ["TB", "HO" + hs], ["G" + q + hs])
+            cp(q, T["G" + hs][:, 16 * a:16 * b], T.TB[:, :].indirect(T["HO" + hs][:, a:b]), ["TB", "HO" + hs], ["G%s%s%d" % (q, hs, part)])
 
     def update(t, h):
         hs, o0 = str(h), 16 * t + 6 * h + 2
@@ -341,17 +350,16 @@ def rank_program(g, core, T, topo):
         ts(T.DL[:, d0 + 18 * m:d0 + 18 * m + 16], T["PK" + hs][:, 18 * m:18 * m + 16], T["S" + hs][:, 18 * m + 15:18 * m + 16],
            T.DD[:, 4 * h + m:4 * h + m + 1], A.is_equal, A.mult, ["PK" + hs, "S" + hs, "DD" + hs, "DLz"], ["DL%d_%d_%d" % (t, h, m)])
 
-    def apply(t, h):
-        for s in range(3):
+    def apply(t, h, ss=range(3)):
+        for s in ss:
             x0, o0, n0 = BK * (2 + 3 * h + s), 48 * t + 16 * s + 6 * h + 2, 192 * t + 64 * s + 32 * h
             cp("v", T.X[:, x0:x0 + BK].indirect(T.OL[:, o0:o0 + 2]), T.VL[:, n0:n0 + 32],
                ["L%d_%d" % (t, h)] + ["Xe%d" % k for k in range(16)], ["Xx%d_%d" % (h, s)])
 
-    def pack(own, ks, q):
-        x0, x1, v0, v1 = (0, 2 * BK, 0, 1024) if own else (2 * BK, 8 * BK, 1024, 4096)
-        rd = ["X0", "X1"] if own else ["Xx%d_%d" % (h, s) for h in (0, 1) for s in range(3)]
+    def pack(ks, q):
+        rd = ["Xx%d_%d" % (h, s) for h in (0, 1) for s in range(3)]
         for k in ks:
-            cp(q, T.VI[:, v0 + k:v1:16], T.X[:, x0 + k + 2:x1:RW], rd, ["O%d_%d" % (own, k)])
+            cp(q, T.VI[:, 1024 + k:4096:16], T.X[:, 2 * BK + k + 2:8 * BK:RW], rd, ["O0_%d" % k])
 
     def store(h, s, qs, rd):
         d = R0 if s is None else 32 * peers[s]
@@ -359,6 +367,11 @@ def rank_program(g, core, T, topo):
         for t in range(4):
             c0 = 2048 * h + 512 * t
             dma(qs[t % len(qs)], "out", T.yv[d:d + 32, c0:c0 + 512], T.VI[32 * t:32 * t + 32, v0:v0 + 512], rd, [])
+
+    def own(h):
+        for k in range(16):
+            cp("s", T.VI[:, 512 * h + k:512 * h + 512:16], T.X[:, BK * h + k + 2:BK * h + BK:RW], ["X%d" % h], ["O1_%d_%d" % (h, k)])
+        store(h, None, "y", ["O1_%d_%d" % (h, k) for k in range(16)])
 
     def finish(h, qs):
         hs = str(h)
@@ -391,7 +404,6 @@ def rank_program(g, core, T, topo):
         gather("v", 0, h)
         gather("s", 0, h)
 
-    later = []
     spread = {(0, 1): range(0, 4), (1, 0): range(4, 8), (1, 1): range(8, 12), (2, 0): range(12, 16)}
     for t in range(RO):
         last = t == RO - 1
@@ -399,11 +411,8 @@ def rank_program(g, core, T, topo):
             hs = str(h)
             PK, S, G = T["PK" + hs], T["S" + hs], T["G" + hs]
             for e in range(16):
-                mm(PK[:, 0:68], G[:, e:2048:16], T.SEL[:, 0:68], False, e == 15, ["Gs" + hs, "Gv" + hs, "SEL"], ["PK" + hs])
-            while later:
-                u, x = later.pop()
-                keybase(u + 1, x)
-                opens(x, u + 2 < RO)
+                mm(PK[:, 0:68], G[:, e:2048:16], T.SEL[:, 0:68], False, e == 15,
+                   ["Gs%s0" % hs, "Gv%s0" % hs, "Gv%s1" % hs, "SEL"], ["PK" + hs])
             op("v", lambda: V.tensor_tensor_scan(S[:, 0:68], T.D0[:, 0:68], PK[:, 0:68], 0.0, A.add, A.max), ["D0", "PK" + hs], ["S" + hs])
             f0 = 8 * (2 * t + 2 + h)
             fk = "F%d_%d" % (t + 1, h)
@@ -413,20 +422,24 @@ def rank_program(g, core, T, topo):
             pick(t, h, T.F[:, f0:f0 + 6], fk)
             if not last:
                 places1(h)
+                update(t, h)
                 places2(h, lambda m: labels(t, h, m))
                 later.append((t, h))
                 gather("s", t + 1, h)
-                update(t, h)
                 gather("v", t + 1, h)
+                fill.append(lambda u=t + 1, x=h: gather("v", u, x, 1))
+                early = t == RO - 2
                 x0 = BK * h
-                cp("g", T.X[:, x0 + 1:x0 + BK:RW], T.X[:, x0 + 17:x0 + BK:RW], ["X" + hs], ["Xl" + hs])
-                cp("g", T.X[:, x0 + 18:x0 + BK:RW], T.X[:, x0 + 2:x0 + BK:RW], ["X" + hs], ["Xr" + hs])
-                if h == 1:
-                    send(T.OFF[:, 16 * t:16 * t + 12], lambda s: T.OL[:, 48 * t + 16 * s:48 * t + 16 * s + 12],
-                         "ax%d" % t, ["OFF%d_0" % t, "OFF%d_1" % t])
-                    send(T.NEW[:, 64 * t:64 * t + 64], lambda s: T.VL[:, 192 * t + 64 * s:192 * t + 64 * s + 64],
-                         "ax%d" % t, ["NEW%d_0" % t, "NEW%d_1" % t])
-                    arrive("ax%d" % t, 2 * allinc, ["L%d_0" % t, "L%d_1" % t])
+                for part in ((1, 0) if early else (0, 1)):
+                    if part == 0:
+                        cp("g", T.X[:, x0 + 1:x0 + BK:RW], T.X[:, x0 + 17:x0 + BK:RW], ["X" + hs], ["Xl" + hs])
+                        cp("g", T.X[:, x0 + 18:x0 + BK:RW], T.X[:, x0 + 2:x0 + BK:RW], ["X" + hs], ["Xr" + hs])
+                    elif h == 1:
+                        send(T.OFF[:, 16 * t:16 * t + 12], lambda s: T.OL[:, 48 * t + 16 * s:48 * t + 16 * s + 12],
+                             "ax%d" % t, ["OFF%d_0" % t, "OFF%d_1" % t])
+                        send(T.NEW[:, 64 * t:64 * t + 64], lambda s: T.VL[:, 192 * t + 64 * s:192 * t + 64 * s + 64],
+                             "ax%d" % t, ["NEW%d_0" % t, "NEW%d_1" % t])
+                        arrive("ax%d" % t, 2 * allinc, ["L%d_0" % t, "L%d_1" % t])
                 for k in spread.get((t, h), []):
                     cp("g", T.X[:, 2 * BK + k + 2:8 * BK:RW], T.VI[:, 1024 + k:4096:16], ["VIx"], ["Xe%d" % k])
             else:
@@ -434,33 +447,39 @@ def rank_program(g, core, T, topo):
                      "af" + hs, ["NEW%d_%d" % (t, h), "MC" + hs])
                 arrive("af" + hs, allinc, ["LF" + hs])
                 mm(T["PA" + hs][:, 0:34], T.SB[:, 128 * h:128 * h + 128], T.CN[:, 0:34], True, False, SBK + ["CN"], ["PA" + hs])
-                update(t, h)
+                for u in range(RO - 1):
+                    d0 = 40 * (2 * u + h)
+                    mm(T["PA" + hs][:, 0:34], T.ID[:, :], T.DL[:, d0:d0 + 34], False, False,
+                       ["ID", "DL%d_%d_0" % (u, h), "DL%d_%d_1" % (u, h)], ["PA" + hs])
                 labels(t, h, 0)
                 labels(t, h, 1)
-                for u in range(RO):
-                    d0 = 40 * (2 * u + h)
-                    mm(T["PA" + hs][:, 0:34], T.ID[:, :], T.DL[:, d0:d0 + 34], False, u == RO - 1,
-                       ["ID", "DL%d_%d_0" % (u, h), "DL%d_%d_1" % (u, h)], ["PA" + hs])
+                d0 = 40 * (2 * t + h)
+                mm(T["PA" + hs][:, 0:34], T.ID[:, :], T.DL[:, d0:d0 + 34], False, True,
+                   ["ID", "DL%d_%d_0" % (t, h), "DL%d_%d_1" % (t, h)], ["PA" + hs])
+                update(t, h)
+                own(h)
                 for m in (0, 1):
                     c0, k0 = 64 * r + 32 * m + h, 40 * h + 18 * m
                     tt(T.NL[:, c0:c0 + 31:2], T["PA" + hs][:, 18 * m:18 * m + 16], T.CAP[:, k0:k0 + 16], A.min,
                        ["PA" + hs, "CAP" + hs], ["NL%d_%d" % (h, m)])
             if (t, h) in JOBS:
-                apply(JOBS[(t, h)], 0)
-                apply(JOBS[(t, h)], 1)
+                j = JOBS[(t, h)]
+                apply(j, 0)
+                if last:
+                    apply(j, 1)
+                    fill.append(lambda: apply(RO - 2, 0, [0, 1]))
+                else:
+                    apply(j, 1, [0])
+                    fill.append(lambda j=j: apply(j, 1, [1, 2]))
 
     NLK = ["NL0_0", "NL0_1", "NL1_0", "NL1_1"]
     send(T.NL[:, 64 * r:64 * r + 64], lambda s: T.NL[:, 64 * r:64 * r + 64], "an", NLK)
     arrive("an", allinc, ["NLx"])
-    pack(1, range(16), "s")
-    OWN = ["O1_%d" % k for k in range(16)]
-    store(0, None, "y", OWN)
-    store(1, None, "y", OWN)
-    apply(RO - 2, 0)
+    apply(RO - 2, 0, [2])
     apply(RO - 2, 1)
-    pack(0, range(0, 2), "g")
-    pack(0, range(2, 6), "s")
-    pack(0, range(6, 16), "v")
+    pack(range(0, 2), "g")
+    pack(range(2, 6), "s")
+    pack(range(6, 16), "v")
     finish(0, "ys")
     finish(1, "ys")
     for h in (0, 1):

@@ -3,29 +3,38 @@ from concourse.mybir import AluOpType as A, ActivationFunctionType as AF
 
 RO = 6
 NP = 2
-RW = 19
+RW = 21
 BK = 32 * RW
-VSH = {(t, h): (16, 8) for t in range(RO) for h in (0, 1)}
-VSH.update({(0, 0): (64, 0), (0, 1): (24, 0), (4, 0): (6, 0), (4, 1): (6, 0), (5, 0): (6, 0)})
-JOBS = {(3, 0): 0, (3, 1): 1, (4, 0): 2, (5, 0): 3}
-FAR = 3088
-PKW = FAR + 512
+MB = 16 * RW
+KW = 70
+MW = 72
+CB = 64
+CUT = {(t, h): (("s", 32), ("s", 32), ("v", 24), ("s", 40)) for t in range(RO) for h in (0, 1)}
+CUT.update({(t, h): (("s", 32), ("s", 32), ("v", 20), ("s", 44)) for t in (3, 4) for h in (0, 1)})
+CUT[0, 0] = (("s", 32), ("v", 32), ("s", 32), ("v", 32))
+BATCH = ((0, 2), (2, 4), (4, 5))
+DUE = {(3, 1): 2, (4, 0): 4, (4, 1): 6, (5, 0): 7, (5, 1): 9}
+NOM = dict(cyc=1.0, pe=0.52, gat=1.3, sca=3.2, lat=40, self=70, wake=120, dma=60, rem=250, fly=1800, slow=3500, byte=0.005, turns=18,
+           shake=300, tab=2500)
+TOP = 557056.0
+PEM = False
+PLAN = {}
 
 SCRATCH = {"ST": ("dram", [6, 128, 512], "bfloat16"), "LD": ("dram", [6, 128, 512], "bfloat16")}
-for _d, _l in (("bfloat16", dict(TB=4096, G0=2048, G1=2048, X=8 * BK, VI=3584 + PKW, WA=64, WZ=512, ID=128, MV=512, SW=256,
-                                 CK=128, SEL=72, CB=72, CI=8, CN=40, BS=8, SB=256, F=128, FI=16, DL=480, Y0=96, Y1=96, DF=64,
-                                 NEW=6 * 64, VL=(RO - 1) * 192, NL=256, MS=96, FL=288)),
-               ("float32", dict(IOT=128, IOM=128, IO3=8, PC=16, QM=4, HA=72, HB=72, CAP=80, D0=72, YI=256, S0=72, S1=72, AL=8,
-                                DD=8, CD=8)),
-               ("int32", dict(PI=8, SI=256, SJ=256, HI0=128, HI1=128, HJ0=128, HJ1=128)),
-               ("uint16", dict(OFF=7 * 16, OL=(RO - 1) * 48, HO0=128, HO1=128, OF=16))):
+for _d, _l in (("bfloat16", dict(TB=4096, G0=2048, G1=2048, X=2 * BK, VI=4096, WA=64, WR=128, WB=1024, ID=128, NID=128,
+                                 ID16=128, MV=512, SW=256, IR=128, SEL=72, CK=72, CI=8, RC=8, RB=40, SB=256, F=64, DL=400,
+                                 Y0=96, Y1=96, DF=64, Z0=80, Z1=80, NS=(RO - 1) * 72, VL=(RO - 1) * 204, DS=256, MS=2 * MW,
+                                 FL=6 * MW, IB=256, CAP=256, SA=256, QB0=128, QB1=128)),
+               ("float32", dict(DD=8, IOT=128, IOG=128, PC=32, GM=8, HA=72, HB=72, HC=72, HD=72, D0=72, YI=256, S0=72, S1=72)),
+               ("int32", dict(PI=8, SI=256, SJ=256, IN=256, HI0=128, HI1=128, HJ0=128, HJ1=128)),
+               ("uint16", dict(OFF=RO * 16, OP=(RO - 1) * 12, HO0=128, HO1=128, OF=16, ON=16))):
     for _n in _l:
         SCRATCH[_n] = ("sbuf", [128, _l[_n]], _d)
 for _h in (0, 1):
-    for _n in ("PA", "PB", "PK", "PS"):
-        SCRATCH["%s%d" % (_n, _h)] = ("psum", [128, 512], "float32")
+    for _n, _w in (("PW", 1024), ("PK", 512), ("PS", 512)):
+        SCRATCH["%s%d" % (_n, _h)] = ("psum", [128, _w], "float32")
 
-SEMAPHORES = (["cv", "cs", "cp", "cg", "sent", "lw", "lsi", "lvo", "lvx", "tb", "aw", "an", "out"]
+SEMAPHORES = (["cv", "cs", "cp", "cg", "sent", "lw", "lsi", "lvo", "lvx", "lin", "tb", "aw", "an", "out"]
               + ["st%d" % k for k in range(NP)] + ["ad%d_%d" % (k, s) for k in range(NP) for s in range(3)]
               + ["ax%d" % t for t in range(RO - 1)] + ["af0", "af1"])
 
@@ -80,7 +89,8 @@ def rank_program(g, core, T, topo):
     def deps(q, rd, wr, skip=None):
         ts = [lastw[k] for k in rd if k in lastw]
         for k in wr:
-            ts += ([lastw[k]] if k in lastw else []) + readers.get(k, [])
+            if k[0] != "~":
+                ts += ([lastw[k]] if k in lastw else []) + readers.get(k, [])
         need(q, [t for t in ts if t is not skip and not (q == "p" and t[0] == "cp")])
 
     def note(tok, rd, wr):
@@ -90,400 +100,506 @@ def rank_program(g, core, T, topo):
             lastw[k] = tok
             readers[k] = []
 
-    def op(q, fn, rd, wr):
-        deps(q, rd, wr)
-        cnt[q] += 1
-        fn().then_inc(T.sem["c" + q], 1)
-        note(["c" + q, cnt[q], dict(clock[q])], rd, wr)
+    calls = []
 
-    def dma(q, name, out, in_, rd, wr):
-        if name not in grp:
-            grp[name] = [name, 0, {}]
-        tok = grp[name]
-        deps(q, rd, wr, tok)
-        Q[q].dma_start(out, in_).then_inc(T.sem[name], 16)
-        tok[1] += 16
-        merge(tok[2], clock[q])
-        note(tok, rd, wr)
+    def op(q, fn, rd, wr, cost):
+        def issue():
+            deps(q, rd, wr)
+            cnt[q] += 1
+            fn().then_inc(T.sem["c" + q], 1)
+            note(["c" + q, cnt[q], dict(clock[q])], rd, wr)
+        calls.append((q, cost, NOM["lat"], rd, wr, None, issue))
 
-    def fused(items, rd):
-        deps("g", rd, [])
-        tr = []
-        for s, eng, src, dst, sem in items:
-            rid, pid = topo.addr(cores[peers[s]])[:2]
-            there = (r - peers[s]) % N - 1
-            tr.append(RemoteDMATransfer(dst_ids=[DstId(rid=rid, pnc=pid)], dma_engine_mask=sum(1 << e for e in eng),
-                                        remote_sem=T.sem[sem(there)], src=src, dst=dst(there)))
-            sent[1] += len(eng)
-        g.remote_dma_fused(tr, local_sem=T.sem.sent)
+    def dma(q, name, out, in_, rd, wr, lat=1500):
+        def issue():
+            tok = grp.setdefault(name, [name, 0, {}])
+            deps(q, rd, wr, tok)
+            Q[q].dma_start(out, in_).then_inc(T.sem[name], 16)
+            tok[1] += 16
+            merge(tok[2], clock[q])
+            note(tok, rd, wr)
+        if name == "out":
+            calls.append((q, NOM["dma"], 0, rd, [">o%d" % len(calls)], name, issue))
+            calls.append(("x", out.shape[0] * out.shape[1] * NOM["byte"], 1000, [">o%d" % (len(calls) - 1)], [], None, lambda: None))
+        else:
+            calls.append((q, NOM["dma"], lat, rd, wr, name, issue))
 
-    def send(src, dst, sem, rd):
-        fused([(s, my[cores[peers[s]]], src, dst, lambda x: sem) for s in order], rd)
+    def fused(items, rd, key):
+        def issue():
+            deps("g", rd, [])
+            tr = []
+            for s, eng, src, dst, sem in items:
+                rid, pid = topo.addr(cores[peers[s]])[:2]
+                there = (r - peers[s]) % N - 1
+                tr.append(RemoteDMATransfer(dst_ids=[DstId(rid=rid, pnc=pid)], dma_engine_mask=sum(1 << e for e in eng),
+                                            remote_sem=T.sem[sem(there)], src=src, dst=dst(there)))
+                sent[1] += len(eng)
+            g.remote_dma_fused(tr, local_sem=T.sem.sent)
+        calls.append(("g", NOM["rem"], 0, rd, [key], "rem", issue))
 
-    def arrive(sem, n, keys):
-        tok = [sem, n, {}]
-        toks.append(tok)
-        note(tok, [], keys)
+    def arrive(sem, n, keys, key, lat):
+        def issue():
+            tok = [sem, n, {}]
+            toks.append(tok)
+            note(tok, [], keys)
+        calls.append(("x", 1, lat, [key], keys, None, issue))
+
+    def send(src, dst, sem, rd, keys, lat=None):
+        fused([(s, my[cores[peers[s]]], src, dst, lambda x: sem) for s in order], rd, ">" + sem)
+        arrive(sem, allinc, keys, ">" + sem, lat or NOM["fly"])
+
+    def plan():
+        n, w, rs, pred, fifo = len(calls), {}, {}, [], {}
+        for j, (q, cost, lat, rd, wr, gp, fn) in enumerate(calls):
+            e = {}
+            for i in [i for k in rd + wr if k[0] != "~" for i in w.get(k, [])] + [i for k in wr for i in rs.get(k, [])]:
+                if gp is None or calls[i][5] != gp:
+                    a = calls[i]
+                    e[i] = a[1] + (0 if a[0] == q == "p" or q == "x" else a[2] + NOM["self" if a[0] == q and not a[5] else "wake"])
+            for i in [i for k in wr if k[0] == "~" for i in w.get(k, [])]:
+                e.setdefault(i, calls[i][1])
+            if gp:
+                if q in fifo:
+                    e.setdefault(fifo[q], calls[fifo[q]][1])
+                fifo[q] = j
+            pred.append(e)
+            for k in rd:
+                rs.setdefault(k, []).append(j)
+            for k in wr:
+                w[k] = [i for i in w.get(k, []) if gp and calls[i][5] == gp] + [j]
+                rs[k] = []
+        tail = [c[1] + c[2] for c in calls]
+        for j in range(n - 1, -1, -1):
+            for i, d in pred[j].items():
+                tail[i] = max(tail[i], d + tail[j])
+        succ = [{} for c in calls]
+        for j in range(n):
+            for i, d in pred[j].items():
+                succ[i][j] = d - calls[i][1] + calls[j][1]
+
+        def fit(rank, before, first):
+            start, busy = [0] * n, {}
+            for j in sorted(range(n), key=lambda j: rank[j]):
+                q, cost = calls[j][:2]
+                t = max([start[i] + d for i, d in before[j].items()] + [first[j]])
+                line = busy.setdefault(q, [])
+                k = len(line)
+                while k and line[k - 1][1] > t:
+                    k -= 1
+                while k < len(line) and line[k][0] < t + cost:
+                    t = max(t, line[k][1])
+                    k += 1
+                line.insert(k, (t, t + cost))
+                start[j] = t
+            return start
+
+        def order(rank, before):
+            for j in (range(n) if before is pred else range(n - 1, -1, -1)):
+                for i in before[j]:
+                    rank[j] = max(rank[j], rank[i] + 0.001)
+            return rank
+
+        start, best, z = fit([-x for x in tail], pred, [0] * n), PLAN.get(r), [1]
+
+        def noise(a):
+            z[0] = z[0] * 48271 % 2147483647
+            return a * (z[0] / 2147483647.0 - 0.5)
+
+        for k in range(0 if best else NOM["turns"]):
+            end = max(start[j] + calls[j][1] + calls[j][2] for j in range(n))
+            if best is None or end < best[0]:
+                best = (end, start)
+            a = NOM["shake"] if k % 3 == 2 else 0
+            if a:
+                start = best[1]
+            back = fit(order([-start[j] - calls[j][1] + noise(a) for j in range(n)], succ), succ, [c[2] for c in calls])
+            start = fit([-back[j] - calls[j][1] for j in range(n)], pred, [0] * n)
+        PLAN[r] = best
+        for j in sorted(range(n), key=lambda j: (best[1][j], j)):
+            calls[j][6]()
 
     V = g.vector
 
+    def cyc(out, *ins):
+        two = all("16" in str(a.dtype) for a in (out,) + ins)
+        return NOM["cyc"] * max(64, out.shape[1] * (0.5 if two else 1))
+
     def ts(out, in0, s1, s2, o0, o1, rd, wr):
         if o1 is None:
-            op("v", lambda: V.tensor_scalar(out, in0, s1, None, o0), rd, wr)
+            op("v", lambda: V.tensor_scalar(out, in0, s1, None, o0), rd, wr, cyc(out, in0))
         else:
-            op("v", lambda: V.tensor_scalar(out, in0, s1, s2, o0, o1), rd, wr)
+            op("v", lambda: V.tensor_scalar(out, in0, s1, s2, o0, o1), rd, wr, cyc(out, in0))
 
     def tt(out, a, b, o, rd, wr):
-        op("v", lambda: V.tensor_tensor(out, a, b, o), rd, wr)
+        op("v", lambda: V.tensor_tensor(out, a, b, o), rd, wr, NOM["cyc"] * max(64, 2 * out.shape[1]))
 
     def cp(q, out, in_, rd, wr):
+        n = out.shape[1]
         if q == "v":
-            op(q, lambda: V.tensor_copy(out, in_), rd, wr)
+            op(q, lambda: V.tensor_copy(out, in_), rd, wr, cyc(out, in_))
         elif q == "s":
-            op(q, lambda: g.scalar.activation(out, in_, AF.Copy), rd, wr)
+            op(q, lambda: g.scalar.activation(out, in_, AF.Copy), rd, wr, NOM["cyc"] * max(64, n))
         else:
-            n = out.shape[1]
-            op(q, lambda: g.affine_select(out, in_, [[0, n]], A.is_equal, 0.0, 0, 0), rd, wr)
+            op(q, lambda: g.affine_select(out, in_, [[0, n]], A.is_equal, 0.0, 0, 0), rd, wr, 170 + 2 * n * NOM["cyc"])
+
+    def pick(q, out, win, off, rd, wr):
+        cost = 60 + NOM["gat"] * out.shape[1]
+        if q == "v":
+            op(q, lambda: V.tensor_copy(out, win.indirect(off)), rd, wr, cost)
+        else:
+            op(q, lambda: g.scalar.activation(out, win.indirect(off), AF.Copy), rd, wr + ["~s"], cost)
+
+    def put(win, off, a, b, rd, wr):
+        cost = 50 + NOM["sca"] * a.shape[1]
+        if b is None:
+            op("v", lambda: V.tensor_copy(win.indirect(off), a), rd, wr, cost)
+        else:
+            op("v", lambda: V.tensor_tensor(win.indirect(off), a, b, A.add), rd, wr, cost)
 
     def ms(out, val, wr):
-        op("v", lambda: V.memset(out, val), [], wr)
+        op("v", lambda: V.memset(out, val), [], wr, cyc(out))
 
     def mm(out, lhsT, rhs, start, stop, rd, wr):
-        op("p", lambda: g.tensor.matmul(out, lhsT, rhs, start, stop), rd, wr)
+        op("p", lambda: g.tensor.matmul(out, lhsT, rhs, start, stop), rd, wr, NOM["pe"] * max(min(64, out.shape[0]), out.shape[1]))
+
+    def iota(out, pattern, channel, wr):
+        fl = {} if "int" in str(out.dtype) else {"allow_small_or_imprecise_dtypes": True}
+        op("g", lambda: g.iota(out, pattern, 0, channel, **fl), [], wr, 130 + 2 * out.shape[1] * NOM["cyc"])
+
+    def scan(t, h):
+        S, PK = T["S%d" % h], T["PK%d" % h]
+        op("v", lambda: V.tensor_tensor_scan(S[:, 0:KW], T.D0[:, 0:KW], PK[:, 0:KW], 0.0, A.add, A.max), ["D0", "PK%d" % h],
+           ["S%d" % h] + ["~a%d" % k for k in range(DUE.get((t, h), 0))], NOM["cyc"] * KW)
 
     R0 = 32 * r
-    dma("y", "lw", T.WA[:, 16 * r:16 * r + 16], T.wt[:, :], [], ["WAo"])
+
+    P = {}
+    for h in (0, 1):
+        P.update({"PA%d" % h: T["PW%d" % h][:, 0:512], "PB%d" % h: T["PW%d" % h][:, 512:1024]})
+
+    def block(s, h, qs, sem, rd, wr, lat=1500):
+        d, v0 = 32 * (peers + [r])[s], 1024 * s + 512 * h
+        for t in range(4):
+            c0, sb = 2048 * h + 512 * t, T.VI[32 * t:32 * t + 32, v0:v0 + 512]
+            if sem == "out":
+                dma(qs[t % len(qs)], sem, T.yv[d:d + 32, c0:c0 + 512], sb, rd, wr)
+            else:
+                dma(qs[t % len(qs)], sem, sb, T.v[d:d + 32, c0:c0 + 512], rd, wr, lat)
+
+    dma("y", "lw", T.WA[:, 16 * r:16 * r + 16], T.wt[:, :], [], ["WAo"], 1200)
     for q, s, k, c in (("s", far[0], 0, 0), ("y", far[1], 0, 0), ("s", far[0], 1, 1), ("y", far[1], 1, 1),
                        ("s", near, 0, 1), ("y", near, 1, 1)):
         d = 32 * peers[s] + 16 * k
-        dma(q, "st%d" % c, T.ST[2 * s + k], T.dem[d:d + 16, :], [], ["ST%d" % c])
-    dma("s", "lsi", T.SI[0:32, :], T.sup[R0:R0 + 32, :], [], ["SI"])
-    dma("y", "lsi", T.SI[32:64, :], T.sup[R0:R0 + 32, :], [], ["SI"])
-    dma("s", "lsi", T.SI[64:96, :], T.inv[R0:R0 + 32, :], [], ["SI"])
+        dma(q, "st%d" % c, T.ST[2 * s + k], T.dem[d:d + 16, :], [], ["ST%d" % c], 1700 + 1200 * c)
+    dma("s", "lsi", T.SI[64:96, :], T.inv[R0:R0 + 32, :], [], ["SI"], 2800)
+    dma("s", "lsi", T.SI[0:32, :], T.sup[R0:R0 + 32, :], [], ["SI"], 2800)
+    dma("y", "lsi", T.SI[32:64, :], T.sup[R0:R0 + 32, :], [], ["SI"], 2800)
     for h in (0, 1):
-        for t in range(4):
-            c0 = 2048 * h + 512 * t
-            dma("ys"[t % 2], "lvo", T.VI[32 * t:32 * t + 32, 512 * h:512 * h + 512], T.v[R0:R0 + 32, c0:c0 + 512], [], ["VIo"])
-    dma("y", "tb", T.TB[R0:R0 + 32, :], T.dem[R0:R0 + 32, :], ["ST1"], ["TB"])
+        block(3, h, "ys", "lvo", [], ["VIo"], 3000)
+    dma("y", "lin", T.IN[:, :], T.inv[:, :], [], ["IN"], 3000)
+    for m in (0, 1):
+        d = 64 * m + 16 * r
+        dma("y", "tb", T.TB[d:d + 16, :], T.dem[R0 + 16 * m:R0 + 16 * m + 16, :], ["ST1"], ["TB"])
 
-    fl = {"allow_small_or_imprecise_dtypes": True}
-    op("g", lambda: g.iota(T.PI[:, 0:1], [[0, 1]], 0, 1), [], ["PI0"])
-    op("g", lambda: g.iota(T.IOT[:, :], [[1, 128]], 0, 0, **fl), [], ["IOT"])
-    op("g", lambda: g.iota(T.IOM[:, :], [[0, 4], [1, 32]], R0, 0, **fl), [], ["IOM"])
-    op("g", lambda: g.iota(T.IO3[:, 0:6], [[1, 2], [0, 3]], 4, 0, **fl), [], ["IO3"])
-    send(T.WA[:, 16 * r:16 * r + 16], lambda s: T.WA[:, 16 * r:16 * r + 16], "aw", ["WAo"])
-    arrive("aw", allinc, ["WAx"])
+    iota(T.PI[:, 0:1], [[0, 1]], 1, ["PI0"])
+    iota(T.IOT[:, :], [[1, 128]], 0, ["IOT"])
+    iota(T.IOG[:, :], [[0, 8], [1, 16]], 0, ["IOG"])
+    send(T.WA[:, 16 * r:16 * r + 16], lambda s: T.WA[:, 16 * r:16 * r + 16], "aw", ["WAo"], ["WAx"], 3000)
 
     def piece(s, k, eng):
         return (s, eng, T.ST[2 * s + k], lambda x: T.LD[2 * x + k], lambda x: "ad%d_%d" % (k, x))
 
     en = my[cores[peers[near]]]
-    fused([piece(s, 0, my[cores[peers[s]]]) for s in far], ["ST0"])
+    fused([piece(s, 0, my[cores[peers[s]]]) for s in far], ["ST0"], ">t0")
     fused([piece(s, 1, my[cores[peers[s]]]) for s in far]
-          + [piece(near, 0, en[:len(en) // 2]), piece(near, 1, en[len(en) // 2:])], ["ST1"])
-    for q, s, k in (("s", far[0], 0), ("y", far[1], 0), ("s", near, 0), ("y", near, 1), ("s", far[0], 1), ("y", far[1], 1)):
+          + [piece(near, 0, en[:len(en) // 2]), piece(near, 1, en[len(en) // 2:])], ["ST1"], ">t1")
+    for q, s, k in (("y", far[0], 0), ("y", far[1], 0), ("y", near, 0), ("y", near, 1), ("y", far[0], 1), ("y", far[1], 1)):
         key = "ad%d_%d" % (k, s)
-        arrive(key, inc[peers[s]] // (2 if s == near else 1), [key])
-        d = 32 * peers[s] + 16 * k
+        arrive(key, inc[peers[s]] // (2 if s == near else 1), [key], ">t%d" % (k or s == near), NOM["tab"])
+        d = 64 * k + 16 * peers[s]
         dma(q, "tb", T.TB[d:d + 16, :], T.LD[2 * s + k], [key], ["TB"])
     for h in (0, 1):
         for s in range(3):
-            for t in range(4):
-                c0 = 2048 * h + 512 * t
-                b0 = 1024 + 1536 * h + 512 * s
-                dma("y", "lvx", T.VI[32 * t:32 * t + 32, b0:b0 + 512], T.v[32 * peers[s]:32 * peers[s] + 32, c0:c0 + 512], ["TB"], ["VIx"])
+            block(s, h, "y", "lvx", ["TB"], ["VIx"])
 
     PC = T.PC
     ts(T.PI[:, 1:2], T.PI[:, 0:1], 4, 1, A.arith_shift_right, A.bitwise_and, ["PI0"], ["PI1"])
     ts(T.PI[:, 2:3], T.PI[:, 0:1], 15, None, A.bitwise_and, None, ["PI0"], ["PI2"])
-    ts(T.PI[:, 3:4], T.PI[:, 0:1], 5, None, A.arith_shift_right, None, ["PI0"], ["PI3"])
+    ts(T.PI[:, 3:4], T.PI[:, 0:1], 6, None, A.arith_shift_right, None, ["PI0"], ["PI3"])
     ts(T.PI[:, 4:5], T.PI[:, 0:1], 4, None, A.arith_shift_right, None, ["PI0"], ["PI4"])
-    ms(T.CK[:, :], 0.0, ["CK"])
-    ms(T.D0[:, :], 0.0, ["D0"])
-    ms(T.BS[:, :], 0.0, ["BS"])
-    ms(T.AL[:, :], 1.0, ["AL0", "AL1"])
-    ms(T.DL[:, :], 0.0, ["DLz"])
-    ms(T.X[:, 0:2 * BK:RW], 100.0, ["Xp"])
-    ms(T.SB[96:128, :], 1.0, ["SB3"])
-    ms(PC[0:32, 10:12], -65536.0, ["sa0"])
-    ms(PC[32:64, 10:12], -512.0, ["sa1"])
-    ms(PC[64:96, 10:11], 1.0, ["sa2"])
-    ms(PC[64:96, 11:12], 0.0, ["sa2b"])
     cp("v", PC[:, 0:5], T.PI[:, 0:5], ["PI0", "PI1", "PI2", "PI3", "PI4"], ["PC"])
-    p_, pm, pi, qd, gr = [PC[:, k:k + 1] for k in range(5)]
-    ms(T.D0[:, 0:19:18], -67108864.0, ["D0"])
-    ms(T.BS[:, 1:6:2], 16.0 * RW, ["BS"])
+    p_, pm, pi, tm, gr = [PC[:, k:k + 1] for k in range(5)]
+    ms(T.D0[:, :], 0.0, ["D0"])
+    ms(T.D0[:, 0:55:18], -67108864.0, ["D0"])
+    ms(T.D0[:, 16:18], 1.0, ["D0"])
+    ms(T.D0[:, 34:36], 1.0, ["D0"])
+    ms(T.DL[:, :], 0.0, ["DLz"])
+    ms(T.Z0[:, :], 0.0, ["Z0z"])
+    ms(T.Z1[:, :], 0.0, ["Z1z"])
+    ms(T.X[:, 1:2 * BK:RW], 100.0, ["Xk1"])
+    ms(T.X[:, 2:2 * BK:RW], 100.0, ["Xk2"])
+    cp("v", T.IR[0:32, :], T.IOG[0:32, :], ["IOG"], ["IR0"])
+    ms(T.IR[32:64, :], 1.0, ["IR1"])
+    ms(T.RC[0:32, 0:2], RW / 32.0, ["RC0"])
+    ms(T.RC[32:64, 0:1], 8.0 * MB / 32, ["RC1"])
+    ms(T.RC[32:64, 1:2], -7.0 * MB / 32, ["RC2"])
+    ms(T.RB[0:32, :], -RW / 32.0, ["RB0"])
+    ms(T.RB[32:64, 0:18], 0.0, ["RB1"])
+    ms(T.RB[32:64, 18:36], -MB / 32.0, ["RB2"])
+    IRK = ["IR0", "IR1"]
     ts(PC[:, 5:6], pm, 1000.0, p_, A.mult, A.add, ["PC"], ["ca"])
     ts(PC[:, 6:7], pm, -1000.0, p_, A.mult, A.add, ["PC"], ["cb"])
     ts(PC[:, 7:8], pm, 18.0, pi, A.mult, A.add, ["PC"], ["cA"])
-    ts(PC[:, 8:9], pm, 16.0, pi, A.mult, A.add, ["PC"], ["cB"])
-    ts(PC[:, 9:10], pi, float(RW), None, A.mult, None, ["PC"], ["base"])
-    ts(PC[96:128, 10:11], PC[96:128, 2:3], -32.0, 480.0, A.mult, A.add, ["PC"], ["sa3"])
-    ts(PC[96:128, 11:12], PC[96:128, 2:3], -32.0, 480.0, A.mult, A.add, ["PC"], ["sa3b"])
-    ts(PC[:, 12:13], pi, 16.0, -2.0, A.mult, A.add, ["PC"], ["pb0"])
-    ts(PC[:, 13:14], pi, 16.0, 254.0, A.mult, A.add, ["PC"], ["pb1"])
-    ms(T.D0[:, 36:53:16], -67108864.0, ["D0"])
+    ts(PC[:, 8:9], tm, 18.0, pi, A.mult, A.add, ["PC"], ["cT"])
+    ts(PC[:, 9:10], pi, float(RW), MB / 2.0, A.mult, A.add, ["PC"], ["base"])
     ca, cb = PC[:, 5:6], PC[:, 6:7]
-    ts(T.SW[:, 0:128], T.IOM[:, :], ca, None, A.is_equal, None, ["IOM", "ca"], ["SW0"])
-    ts(T.SW[:, 128:256], T.IOM[:, :], -1000.0, cb, A.add, A.is_equal, ["IOM", "cb"], ["SW1"])
-    ts(T.CI[:, 0:6], T.IO3[:, 0:6], gr, -1.0, A.is_equal, A.mult, ["IO3", "PC"], ["CI"])
-    ts(T.QM[:, :], T.IOT[:, 0:4], qd, None, A.is_equal, None, ["IOT", "PC"], ["QM"])
+    for m in (0, 1):
+        ts(T.SW[:, 128 * m:128 * m + 128], T.IOG[:, :], R0 + 16.0 * m, p_, A.add, A.is_equal, ["IOG", "PC"], ["SW%d" % m])
+    ts(T.CI[:, 0:2], T.IOT[:, 4:6], gr, -1.0, A.is_equal, A.mult, ["IOT", "PC"], ["CI"])
+    ts(T.GM[:, :], T.IOT[:, 0:8], gr, None, A.is_equal, None, ["IOT", "PC"], ["GM"])
     ts(T.ID[:, :], T.IOT[:, :], p_, None, A.is_equal, None, ["IOT", "PC"], ["ID"])
-    ms(T.D0[:, 16:18], 1.0, ["D0"])
+    ts(T.ID16[:, :], T.IOT[:, :], p_, 16.0, A.is_equal, A.mult, ["IOT", "PC"], ["ID16"])
+    ts(T.NID[:, :], T.IOT[:, :], p_, -1.0, A.is_equal, A.mult, ["IOT", "PC"], ["NID"])
     ts(T.MV[:, 0:128], T.IOT[:, :], ca, None, A.is_equal, None, ["IOT", "ca"], ["MV0"])
     ts(T.MV[:, 128:256], T.IOT[:, :], -984.0, cb, A.add, A.is_equal, ["IOT", "cb"], ["MV1"])
     ts(T.MV[:, 256:384], T.IOT[:, :], -16.0, ca, A.add, A.is_equal, ["IOT", "ca"], ["MV2"])
     ts(T.MV[:, 384:512], T.IOT[:, :], -1000.0, cb, A.add, A.is_equal, ["IOT", "cb"], ["MV3"])
-    ms(T.D0[:, 34:36], 1.0, ["D0"])
-    ts(T.HA[:, :], T.IOT[:, 0:72], PC[:, 7:8], None, A.is_equal, None, ["IOT", "cA"], ["HA"])
-    ts(T.HB[:, :], T.IOT[:, 0:72], -36.0, PC[:, 8:9], A.add, A.is_equal, ["IOT", "cB"], ["HB"])
-    ts(T.CN[:, 0:34], T.HA[:, 0:34], T.QM[:, 2:3], None, A.mult, None, ["HA", "QM"], ["CN"])
-    tt(T.S0[:, :], T.HA[:, :], T.HB[:, :], A.add, ["HA", "HB"], ["S0"])
-    sas = ["sa0", "sa1", "sa2", "sa2b", "sa3", "sa3b"]
-    ts(T.HA[:, :], T.HA[:, :], PC[:, 10:11], None, A.mult, None, ["HA"] + sas, ["HA"])
-    ts(T.HB[:, :], T.HB[:, :], PC[:, 11:12], None, A.mult, None, ["HB"] + sas, ["HB"])
-    ts(T.SEL[:, :], T.S0[:, :], 512.0, None, A.mult, None, ["S0"], ["SEL"])
-    tt(T.CB[:, :], T.HA[:, :], T.HB[:, :], A.add, ["HA", "HB"], ["CB"])
+    ms(T.SB[96:128, :], 1.0, ["SB3"])
+    ts(T.SA[64:96, :], T.SI[64:96, :], 0.0, 2.0, A.is_ge, A.mult, ["SI"], ["SA"])
+    ts(T.SB[64:96, :], T.SI[64:96, :], 1.0, None, A.add, None, ["SI"], ["SB2"])
+    tt(T.SB[64:96, :], T.SB[64:96, :], T.SA[64:96, :], A.add, ["SA", "SB2"], ["SB2"])
     ts(T.SJ[0:32, :], T.SI[0:32, :], 7, None, A.arith_shift_right, None, ["SI"], ["SJ0"])
     ts(T.SJ[32:64, :], T.SI[32:64, :], 127, None, A.bitwise_and, None, ["SI"], ["SJ1"])
-    ms(T.CB[96:128, 16:18], -1048576.0, ["CB"])
-    ts(T.SB[64:96, :], T.SI[64:96, :], 1.0, None, A.add, None, ["SI"], ["SB2"])
-    ms(T.CB[96:128, 34:36], -1048576.0, ["CB"])
     cp("v", T.SB[0:64, :], T.SJ[0:64, :], ["SJ0", "SJ1"], ["SB0"])
     SBK = ["SB0", "SB2", "SB3"]
+    ms(PC[0:32, 10:12], -65536.0, ["sa0"])
+    ms(PC[32:64, 10:12], -512.0, ["sa1"])
+    ms(PC[64:96, 10:11], 1.0, ["sa2"])
+    ms(PC[64:96, 11:12], 0.0, ["sa2b"])
+    ts(PC[96:128, 10:11], PC[96:128, 2:3], -32.0, 480.0, A.mult, A.add, ["PC"], ["sa3"])
+    ts(PC[96:128, 11:12], PC[96:128, 2:3], -32.0, 480.0, A.mult, A.add, ["PC"], ["sa3b"])
+    sas = ["sa0", "sa1", "sa2", "sa2b", "sa3", "sa3b"]
+    ts(T.HA[:, :], T.IOT[:, 0:72], PC[:, 7:8], PC[:, 10:11], A.is_equal, A.mult, ["IOT", "cA"] + sas, ["HA"])
+    ts(T.HB[:, :], T.IOT[:, 0:72], -36.0, PC[:, 7:8], A.add, A.is_equal, ["IOT", "cA"], ["HB"])
+    ts(T.HB[:, :], T.HB[:, :], PC[:, 11:12], None, A.mult, None, ["HB"] + sas, ["HB"])
+    tt(T.CK[:, :], T.HA[:, :], T.HB[:, :], A.add, ["HA", "HB"], ["CK"])
+    ms(T.CK[96:128, 16:18], -1048576.0, ["CK"])
+    ms(T.CK[96:128, 34:36], -1048576.0, ["CK"])
+    ts(T.HC[:, :], T.IOT[:, 0:72], PC[:, 8:9], 512.0, A.is_equal, A.mult, ["IOT", "cT"], ["HC"])
+    cp("v", T.SEL[:, 0:36], T.HC[:, 0:36], ["HC"], ["SEL0"])
+    cp("v", T.SEL[:, 36:72], T.HC[:, 0:36], ["HC"], ["SEL1"])
+    ts(PC[:, 12:13], pm, float(MB), 3.0 - MB / 2, A.mult, A.add, ["PC"], ["pk0"])
+    ts(PC[:, 13:14], pi, 16.0, PC[:, 12:13], A.mult, A.subtract, ["PC", "pk0"], ["pk1"])
+    for k in range(4):
+        ts(PC[:, 14 + k:15 + k], PC[:, 13:14], 256.0 * k, None, A.add, None, ["pk1"], ["pk%d" % (2 + k)])
+    PKK = ["pk%d" % k for k in range(6)]
+    cp("v", T.IB[:, :], T.IN[:, :], ["IN"], ["IB"])
+    ts(T.CAP[:, :], T.IN[:, :], 16.0, 15.0, A.mult, A.add, ["IN"], ["CAP"])
+    for x in range(N):
+        for m in (0, 1):
+            mm(T.PK0[:, 64 * m + 16 * x:64 * m + 16 * x + 16], T.SW[:, 128 * m:128 * m + 128], T.WA[:, 16 * x:16 * x + 16],
+               True, True, ["SW%d" % m, "WAo", "WAx"], ["PK0"])
+    cp("v", T.WR[:, :], T.PK0[:, 0:128], ["PK0"], ["WR"])
+    for k in range(8):
+        ts(T.WB[:, k:1024:8], T.WR[:, :], T.GM[:, k:k + 1], None, A.mult, None, ["WR", "GM"], ["WB%d" % k])
+    WBK = ["WB%d" % k for k in range(8)]
     for h in (0, 1):
-        mm(T["PS%d" % h][:, 8:14], T.SB[:, 128 * h:128 * h + 128], T.CI[:, 0:6], True, True, SBK + ["CI"], ["PS%d" % h])
-        mm(T["PS%d" % h][:, 16:50], T.SB[:, 128 * h:128 * h + 128], T.CN[:, 0:34], True, True, SBK + ["CN"], ["PS%d" % h])
-    for k in range(16):
-        cp("v", T.X[:, k + 2:2 * BK:RW], T.VI[:, k:1024:16], ["VIo"], ["Xi%d" % k])
-    cp("v", T.X[:, 1:2 * BK:RW], T.VI[:, 15:1024:16], ["VIo"], ["Xi16"])
-    cp("v", T.X[:, 18:2 * BK:RW], T.VI[:, 0:1024:16], ["VIo"], ["Xi17"])
-    XI = ["Xp"] + ["Xi%d" % k for k in range(18)]
-    for h in (0, 1):
-        ts(T.FI[:, 8 * h:8 * h + 6], T["PS%d" % h][:, 8:14], 137.0, None, A.add, None, ["PS%d" % h], ["FI%d" % h])
-        ts(T.F[:, 8 * h:8 * h + 6], T["PS%d" % h][:, 8:14], 136.0, None, A.add, None, ["PS%d" % h], ["F0_%d" % h])
-        ts(T.CAP[:, 40 * h:40 * h + 34], T["PS%d" % h][:, 16:50], 0.0, 100.0, A.is_gt, A.mult, ["PS%d" % h], ["CAP%d" % h])
-
-    later, fill = [], []
-
-    def new(t, h):
-        return T.MS[:, 48 * h:48 * h + 32] if t == RO - 1 else T.NEW[:, 64 * t + 32 * h:64 * t + 32 * h + 32]
-
-    def pick(t, h, Fap, fk):
-        PS, Y, hs = T["PS%d" % h], T["Y%d" % h], str(h)
         for m in (0, 1):
             for b in (0, 1):
-                mm(PS[:, b:6:2], T.MV[:, 128 * (2 * m + b):128 * (2 * m + b) + 128], Fap[:, 3 * m:3 * m + 3], False,
-                   b == 1 and m == 1, ["MV%d" % (2 * m + b), fk + "_%d" % m if t < RO else fk], ["PS" + hs])
-        while later:
-            u, x = later.pop()
-            keybase(u + 1, x)
-            opens(x, u + 2 < RO)
-        if t < RO:
-            f0 = 8 * (2 * t + h)
-            tt(T.DD[:, 4 * h:4 * h + 2], T.F[:, f0:f0 + 6:3], Fap[:, 0:6:3], A.subtract,
-               [fk + "_0", fk + "_1"] + (["F0_" + hs] if t == 0 else []), ["DD" + hs])
-            if t < RO - 1:
-                ts(T.AL[:, 4 * h:4 * h + 2], Fap[:, 0:6:3], 0.0, None, A.is_gt, None, [fk + "_0", fk + "_1"], ["AL" + hs])
-            while fill:
-                fill.pop(0)()
-        o0 = 16 * t + 6 * h
-        ok = "OFF%d_%d" % (t, h)
-        ts(T.OFF[:, o0:o0 + 6], PS[:, 0:6], PC[:, 9:10], None, A.add, None, ["PS" + hs, "base"], [ok])
-        fin = t == RO - 1
-        c0 = 4 * h
-        if fin:
-            tt(T.CD[:, c0:c0 + 2], PS[:, 2:4], T.BS[:, 2:4], A.subtract, ["PS" + hs, "BS"], ["CD" + hs])
-        cp("v", Y[:, :], T.X[:, BK * h:BK * h + BK].indirect(T.OFF[:, o0:o0 + 6]), [ok, "X" + hs, "Xl" + hs, "Xr" + hs] + XI, ["Y" + hs])
-        if fin:
-            ts(T.CD[:, c0 + 2:c0 + 4], T.CD[:, c0:c0 + 2], 1.0, float(FAR), A.is_le, A.mult, ["CD" + hs], ["CE" + hs])
-        tt(T.DF[:, 32 * h:32 * h + 32], Y[:, 0:32], Y[:, 32:64], A.subtract, ["Y" + hs], ["DF" + hs])
-        if fin:
-            tt(T.MS[:, 48 * h + 32:48 * h + 34], T.CD[:, c0:c0 + 2], T.CD[:, c0 + 2:c0 + 4], A.add, ["CD" + hs, "CE" + hs], ["MC" + hs])
-        if t < RO:
-            tt(new(t, h), T.DF[:, 32 * h:32 * h + 32], Y[:, 64:96], A.add, ["Y" + hs, "DF" + hs], ["NEW%d_%d" % (t, h)])
+                c0 = 3072 + 512 * h + 256 * b
+                mm(T.PW0[:, 512 * h + 256 * m:512 * h + 256 * m + 256], T.MV[:, 128 * (2 * b + m):128 * (2 * b + m) + 128],
+                   T.VI[:, c0:c0 + 256], b == 0, b == 1, ["MV%d" % (2 * b + m), "VIo"], [("PA0", "PB0")[h]])
+    for k, a in [(k + 4, k) for k in range(16)] + [(0, 0), (3, 15), (20, 0)]:
+        cp("s", T.X[:, k:2 * BK:RW], T.PW0[:, a:1024:16], ["PA0", "PB0"], ["Xi%d" % k])
+    XI = ["Xk1", "Xk2"] + ["Xi%d" % k for k in [0] + list(range(3, RW))]
 
-    def opens(h, places):
-        hs = str(h)
-        mm(T["PS" + hs][:, 0:6], T.ID[:, :], T.BS[:, 0:6], True, False, ["ID", "BS"], ["PS" + hs])
-        if places:
-            mm(T["PA" + hs][:, 0:128], T.ID[:, :], T.CK[:, :], True, False, ["ID", "CK"], ["PA" + hs])
+    def rel(t, h):
+        return T.F[:, 8 * t + 4 * h:8 * t + 4 * h + 2], "F%d_%d" % (t, h)
 
-    def places1(h):
-        hs = str(h)
-        for x, k in ((T["Y" + hs][:, 64:96], "Y"), (T.DF[:, 32 * h:32 * h + 32], "DF")):
-            for q in range(4):
-                mm(T["PA" + hs][:, 32 * q:32 * q + 32], T.WZ[:, 128 * q:128 * q + 128], x, False, k == "DF" and q == 3,
-                   ["WZ%d" % q, k + hs], ["PA" + hs])
+    def cap(t, h):
+        Fap, fk = rel(t, h)
+        mm(P["PB%d" % h][:, 128:130], T.IR[0:64, :], T.RC[0:64, 0:2], True, False, IRK + ["RC0", "RC1", "RC2"], ["PB%d" % h])
+        mm(P["PB%d" % h][:, 128:130], T.ID16[:, :], Fap, False, True, ["ID16", fk], ["PB%d" % h])
 
-    def places2(h, between):
-        hs = str(h)
-        cp("v", T["HI" + hs][:, :], T["PA" + hs][:, 0:128], ["PA" + hs], ["HI" + hs])
-        between(0)
-        ts(T["HJ" + hs][:, :], T["HI" + hs][:, :], 4095, None, A.bitwise_and, None, ["HI" + hs], ["HJ" + hs])
-        between(1)
-        cp("v", T["HO" + hs][:, :], T["HJ" + hs][:, :], ["HJ" + hs], ["HO" + hs])
+    def places(h):
+        hs, Z = str(h), T["Z%d" % h]
+        for c, (bank, a, b) in enumerate((("PA" + hs, 0, CB), ("PB" + hs, CB, 128))):
+            for m in (0, 1):
+                for x in range(N):
+                    p0, z0, w0 = 64 * m + 32 * (x // 2), 32 * m + 16 * (1 - x % 2), 128 * (4 * m + x)
+                    mm(P[bank][p0:p0 + 32, 0:b - a], Z[:, z0:z0 + 32], T.WB[:, w0 + a:w0 + b], m + x == 0 if PEM else x % 2 == 0, x % 2 == 1,
+                       WBK + ["Z%d_%d" % (h, m), "Z%dz" % h], [bank])
+            key = hs + str(c)
+            if PEM:
+                ts(T["QB" + hs][:, a:b], P[bank][:, 0:b - a], TOP - 2047.5, None, A.add, None, [bank], ["QB" + key])
+                mm(P[bank][:, 0:b - a], T.NID[:, :], T["QB" + hs][:, a:b], False, True, ["NID", "QB" + key], [bank])
+                ts(T["HO" + hs][:, a:b], P[bank][:, 0:b - a], TOP, None, A.add, None, [bank], ["HO" + key])
+                continue
+            cp("v", T["HI" + hs][:, a:b], P[bank][:, 0:b - a], [bank], ["HI" + key])
+            ts(T["HJ" + hs][:, a:b], T["HI" + hs][:, a:b], 4095, None, A.bitwise_and, None, ["HI" + key], ["HJ" + key])
+            cp("v", T["HO" + hs][:, a:b], T["HJ" + hs][:, a:b], ["HJ" + key], ["HO" + key])
 
-    def keybase(t, h):
+    def keys(t, h):
         hs = str(h)
-        mm(T["PK" + hs][:, 0:68], T.SB[:, 128 * h:128 * h + 128], T.CB[:, 0:68], True, False, SBK + ["CB"], ["PK" + hs])
+        PK = T["PK" + hs]
+        mm(PK[:, 0:KW], T.SB[:, 128 * h:128 * h + 128], T.CK[:, 0:KW], True, False, SBK + ["CK"], ["PK" + hs])
+        mm(PK[:, 36:KW], T.IR[0:64, :], T.RB[0:64, 0:34], False, False, IRK + ["RB0", "RB1", "RB2"], ["PK" + hs])
         for u in range(t):
             d0 = 40 * (2 * u + h)
-            mm(T["PK" + hs][:, 0:34], T.ID[:, :], T.DL[:, d0:d0 + 34], False, False,
+            mm(PK[:, 0:34], T.ID[:, :], T.DL[:, d0:d0 + 34], False, False,
                ["ID", "DLz", "DL%d_%d_0" % (u, h), "DL%d_%d_1" % (u, h)], ["PK" + hs])
-
-    def gather(q, t, h, part=0):
-        hs = str(h)
-        w = VSH[(t, h)]
-        a = 128 - sum(w[part:])
-        a, b = (0, a) if q == "s" else (a, a + w[part])
-        if a < b:
-            cp(q, T["G" + hs][:, 16 * a:16 * b], T.TB[:, :].indirect(T["HO" + hs][:, a:b]), ["TB", "HO" + hs], ["G%s%s%d" % (q, hs, part)])
-
-    def update(t, h):
-        hs, o0 = str(h), 16 * t + 6 * h + 2
-        cp("v", T.X[:, BK * h:BK * h + BK].indirect(T.OFF[:, o0:o0 + 2]), new(t, h),
-           ["OFF%d_%d" % (t, h), "NEW%d_%d" % (t, h)], ["X" + hs, "Xl" + hs, "Xr" + hs])
+        a, ends = 0, []
+        for q, n in CUT[t, h]:
+            pick(q, T["G" + hs][:, 16 * a:16 * (a + n)], T.TB[:, :], T["HO" + hs][:, a:a + n],
+                 ["TB"] + ["HO%s%d" % (hs, c) for c in {a >= CB, a + n > CB}], ["G%s_%d" % (hs, c) for c in range(a // 4, (a + n) // 4)])
+            a += n
+        for e in range(16):
+            mm(PK[:, 0:KW], T["G" + hs][:, 128 * e:128 * e + 128], T.SEL[:, 0:KW], False, e == 15,
+               ["G%s_%d" % (hs, 2 * e), "G%s_%d" % (hs, 2 * e + 1), "SEL0", "SEL1"], ["PK" + hs])
 
     def labels(t, h, m):
-        hs, d0 = str(h), 40 * (2 * t + h)
-        ts(T.DL[:, d0 + 18 * m:d0 + 18 * m + 16], T["PK" + hs][:, 18 * m:18 * m + 16], T["S" + hs][:, 18 * m + 15:18 * m + 16],
-           T.DD[:, 4 * h + m:4 * h + m + 1], A.is_equal, A.mult, ["PK" + hs, "S" + hs, "DD" + hs, "DLz"], ["DL%d_%d_%d" % (t, h, m)])
+        hs = str(h)
+        if t < RO - 1:
+            d0 = 40 * (2 * t + h) + 18 * m
+            out, dd, k = T.DL[:, d0:d0 + 16], T["PS" + hs][:, 64 + m:65 + m], "PS" + hs
+        else:
+            d0 = MW * h + 34 + 16 * m
+            out, dd, k = T.MS[:, d0:d0 + 16], T.DD[:, 4 * h + m:4 * h + m + 1], "DD" + hs
+        ts(out, T["PK" + hs][:, 18 * m:18 * m + 16], T["S" + hs][:, 18 * m + 15:18 * m + 16], dd, A.is_equal, A.mult,
+           ["PK" + hs, "S" + hs, k, "DLz"], ["DL%d_%d_%d" % (t, h, m)])
 
-    def apply(t, h, ss=range(3)):
-        for s in ss:
-            x0, o0, n0 = BK * (2 + 3 * h + s), 48 * t + 16 * s + 6 * h + 2, 192 * t + 64 * s + 32 * h
-            cp("v", T.X[:, x0:x0 + BK].indirect(T.OL[:, o0:o0 + 2]), T.VL[:, n0:n0 + 32],
-               ["L%d_%d" % (t, h)] + ["Xe%d" % k for k in range(16)], ["Xx%d_%d" % (h, s)])
+    def turn(t, h, what):
+        hs = str(h)
+        Fap, fk = rel(t + 1, h)
+        first = h == 0 or t == RO - 1
+        for b in (0, 1):
+            for m in (0, 1):
+                if what:
+                    c0, n, src, k = 16 * b + (2 if first else 0), 16, T["Z" + hs][:, 16 + 32 * m:32 + 32 * m], "Z%d_%d" % (h, m)
+                else:
+                    c0, n, src, k = b + (0 if first else 32), 1, Fap[:, m:m + 1], fk
+                mm(T["PS" + hs][:, c0:c0 + n], T.MV[:, 128 * (2 * m + b):128 * (2 * m + b) + 128], src, m == 0, m == 1,
+                   ["MV%d" % (2 * m + b), k], ["PS" + hs])
 
-    def pack(ks, q):
-        rd = ["Xx%d_%d" % (h, s) for h in (0, 1) for s in range(3)]
-        for k in ks:
-            cp(q, T.VI[:, 1024 + k:4096:16], T.X[:, 2 * BK + k + 2:8 * BK:RW], rd, ["O0_%d" % k])
-
-    def store(h, s, qs, rd):
-        d = R0 if s is None else 32 * peers[s]
-        v0 = 512 * h if s is None else 1024 + 1536 * h + 512 * s
-        for t in range(4):
-            c0 = 2048 * h + 512 * t
-            dma(qs[t % len(qs)], "out", T.yv[d:d + 32, c0:c0 + 512], T.VI[32 * t:32 * t + 32, v0:v0 + 512], rd, [])
-
-    def own(h):
-        for k in range(16):
-            cp("s", T.VI[:, 512 * h + k:512 * h + 512:16], T.X[:, BK * h + k + 2:BK * h + BK:RW], ["X%d" % h], ["O1_%d_%d" % (h, k)])
-        store(h, None, "y", ["O1_%d_%d" % (h, k) for k in range(16)])
+    def offsets(t0, t1):
+        for h in (0, 1):
+            for b in (0, 1):
+                ts(T.OP[:, 12 * t0 + 2 * h + b:12 * t1:4], T.VL[:, 204 * t0 + 66 * h + b:204 * t1:68],
+                   PC[:, 12:13], PC[:, 14 + 2 * h + b:15 + 2 * h + b], A.max, A.add,
+                   PKK + ["L%d" % t for t in range(t0, t1)], ["OP%d_%d%d" % (t, h, b) for t in range(t0, t1)])
+        for t in range(t0, t1):
+            for s in range(3):
+                put(T.VI[:, 1024 * s:1024 + 1024 * s], T.OP[:, 12 * t + 4 * s:12 * t + 4 * s + 4],
+                    T.VL[:, 204 * t + 68 * s + 2:204 * t + 68 * s + 66], None,
+                    ["L%d" % t, "VIx"] + ["OP%d_%d%d" % (t, h, b) for h in (0, 1) for b in (0, 1)], ["B0_%d" % s, "B1_%d" % s, "~a%d" % (3 * t + s)])
 
     def finish(h, qs):
         hs = str(h)
         for b in (0, 1):
-            f0 = 144 * h + 32 + b
-            ts(T.OF[:, 8 * h + b:8 * h + 6:2], T.FL[:, f0:144 * h + 144:48], PC[:, 12 + b:13 + b], None, A.add, None,
-               ["LF" + hs, "pb%d" % b], ["OF%d_%d" % (h, b)])
+            ts(T.OF[:, 8 * h + b:8 * h + 6:2], T.FL[:, 3 * MW * h + b:3 * MW * (h + 1):MW], PC[:, 12:13], PC[:, 14 + b:15 + b], A.max, A.add,
+               ["LF" + hs] + PKK, ["OF%d_%d" % (h, b)])
         for s in range(3):
-            v0, f0 = 1024 + 1536 * h + 512 * s, 144 * h + 48 * s
-            cp("v", T.VI[:, v0:v0 + PKW].indirect(T.OF[:, 8 * h + 2 * s:8 * h + 2 * s + 2]), T.FL[:, f0:f0 + 32],
-               ["LF" + hs, "OF%d_0" % h, "OF%d_1" % h] + ["O0_%d" % k for k in range(16)], ["VIw", "B%d_%d" % (h, s)])
-            store(h, s, qs, ["B%d_%d" % (h, s)])
+            v0, f0 = 1024 * s + 512 * h, MW * (3 * h + s) + 2
+            put(T.VI[:, v0:v0 + 512], T.OF[:, 8 * h + 2 * s:8 * h + 2 * s + 2], T.FL[:, f0:f0 + 32], None,
+                ["LF" + hs, "OF%d_0" % h, "OF%d_1" % h], ["B%d_%d" % (h, s)])
+            block(s, h, qs, "out", ["B%d_%d" % (h, s)], [])
+
+    def slots(h, q):
+        hs = str(h)
+        PB = T["PK" + hs]
+        mm(PB[:, 0:128], T.ID[:, :], T.IB[:, 128 * h:128 * h + 128], True, False, ["ID", "IB"], ["PK" + hs])
+        for x in range(N):
+            mm(PB[32 * x:32 * x + 32, 0:128], T.DS[:, 64 * x + 32 * h:64 * x + 32 * h + 32], T.ID[:, :], False, False,
+               ["ID", "DS0", "DS1", "DSx"], ["PK" + hs])
+        for k, x in enumerate([r] + peers):
+            src = T.MS[:, MW * h + 34:MW * h + 66] if k == 0 else T.FL[:, MW * (3 * h + k - 1) + 34:MW * (3 * h + k - 1) + 66]
+            mm(PB[32 * x:32 * x + 32, 0:128], src, T.ID[:, :], False, True,
+               ["ID", "DL%d_%d_0" % (RO - 1, h), "DL%d_%d_1" % (RO - 1, h)] + (["LF" + hs] if k else []), ["PK" + hs])
+        tt(T.YI[:, 128 * h:128 * h + 128], PB[:, 0:128], T.CAP[:, 128 * h:128 * h + 128], A.min, ["PK" + hs, "CAP"], ["YI" + hs])
+        dma(q, "out", T.yi[:, 128 * h:128 * h + 128], T.YI[:, 128 * h:128 * h + 128], ["YI" + hs], [])
 
     for h in (0, 1):
-        opens(h, True)
-        pick(RO, h, T.FI[:, 8 * h:8 * h + 6], "FI%d" % h)
-    for x in range(N):
+        hs = str(h)
+        mm(T["PS" + hs][:, 0:2], T.SB[64:96, 128 * h:128 * h + 128], T.CI[64:96, 0:2], True, True, ["SB2", "CI"], ["PS" + hs])
         for m in (0, 1):
-            mm(T.PK0[:, 32 * x + 16 * m:32 * x + 16 * m + 16], T.SW[:, 128 * m:128 * m + 128], T.WA[:, 16 * x:16 * x + 16],
-               True, True, ["SW%d" % m, "WAo", "WAx"], ["PK0"])
-    for q in range(4):
-        ts(T.WZ[:, 128 * q:128 * q + 128], T.PK0[:, 0:128], T.QM[:, q:q + 1], None, A.mult, None, ["PK0", "QM"], ["WZ%d" % q])
-    for h in (0, 1):
-        places1(h)
-    for h in (0, 1):
-        places2(h, lambda k: None)
-        keybase(0, h)
-        opens(h, True)
-    for h in (0, 1):
-        gather("v", 0, h)
-        gather("s", 0, h)
+            ts(T.ON[:, 4 * h + 2 * m:4 * h + 2 * m + 1], T["PS" + hs][:, m:m + 1], PC[:, 9:10], 169.0 + MB * m - MB / 2, A.add, A.add,
+               ["PS" + hs, "base"], ["ON%d_%d" % (h, m)])
+            pick("v", T["Z" + hs][:, 16 + 32 * m:32 + 32 * m], T.X[:, BK * h:BK * h + BK], T.ON[:, 4 * h + 2 * m:4 * h + 2 * m + 1],
+                 ["ON%d_%d" % (h, m), "Z%dz" % h] + XI, ["Z%d_%d" % (h, m)])
+            ts(T.F[:, 4 * h + m:4 * h + m + 1], T["PS" + hs][:, m:m + 1], 168.0 + MB * m - MB / 2, None, A.add, None,
+               ["PS" + hs], ["F0_" + hs])
+        places(h)
+        cap(0, h)
 
-    spread = {(0, 1): range(0, 4), (1, 0): range(4, 8), (1, 1): range(8, 12), (2, 0): range(12, 16)}
     for t in range(RO):
         last = t == RO - 1
         for h in (0, 1):
             hs = str(h)
-            PK, S, G = T["PK" + hs], T["S" + hs], T["G" + hs]
-            for e in range(16):
-                mm(PK[:, 0:68], G[:, e:2048:16], T.SEL[:, 0:68], False, e == 15,
-                   ["Gs%s0" % hs, "Gv%s0" % hs, "Gv%s1" % hs, "SEL"], ["PK" + hs])
-            op("v", lambda: V.tensor_tensor_scan(S[:, 0:68], T.D0[:, 0:68], PK[:, 0:68], 0.0, A.add, A.max), ["D0", "PK" + hs], ["S" + hs])
-            f0 = 8 * (2 * t + 2 + h)
-            fk = "F%d_%d" % (t + 1, h)
+            PS, S, Y, Z = T["PS" + hs], T["S" + hs], T["Y" + hs], T["Z" + hs]
+            DF, XW = T.DF[:, 32 * h:32 * h + 32], T.X[:, BK * h:BK * h + BK]
+            o0, ok = 16 * t + 6 * h, ["OFF%d_%d_%d" % (t, h, m) for m in (0, 1)]
+            (F0, k0), (F1, k1) = rel(t, h), rel(t + 1, h)
+            keys(t, h)
+            scan(t, h)
             for m in (0, 1):
-                ts(T.F[:, f0 + 3 * m:f0 + 3 * m + 3], S[:, 18 * m + 15:18 * m + 18], S[:, 51 + 16 * m:52 + 16 * m],
-                   T.AL[:, 4 * h + m:4 * h + m + 1], A.subtract, A.mult, ["S" + hs, "AL" + hs], [fk + "_%d" % m])
-            pick(t, h, T.F[:, f0:f0 + 6], fk)
-            if not last:
-                places1(h)
-                update(t, h)
-                places2(h, lambda m: labels(t, h, m))
-                later.append((t, h))
-                gather("s", t + 1, h)
-                gather("v", t + 1, h)
-                fill.append(lambda u=t + 1, x=h: gather("v", u, x, 1))
-                early = t == RO - 2
-                x0 = BK * h
-                for part in ((1, 0) if early else (0, 1)):
-                    if part == 0:
-                        cp("g", T.X[:, x0 + 1:x0 + BK:RW], T.X[:, x0 + 17:x0 + BK:RW], ["X" + hs], ["Xl" + hs])
-                        cp("g", T.X[:, x0 + 18:x0 + BK:RW], T.X[:, x0 + 2:x0 + BK:RW], ["X" + hs], ["Xr" + hs])
-                    elif h == 1:
-                        send(T.OFF[:, 16 * t:16 * t + 12], lambda s: T.OL[:, 48 * t + 16 * s:48 * t + 16 * s + 12],
-                             "ax%d" % t, ["OFF%d_0" % t, "OFF%d_1" % t])
-                        send(T.NEW[:, 64 * t:64 * t + 64], lambda s: T.VL[:, 192 * t + 64 * s:192 * t + 64 * s + 64],
-                             "ax%d" % t, ["NEW%d_0" % t, "NEW%d_1" % t])
-                        arrive("ax%d" % t, 2 * allinc, ["L%d_0" % t, "L%d_1" % t])
-                for k in spread.get((t, h), []):
-                    cp("g", T.X[:, 2 * BK + k + 2:8 * BK:RW], T.VI[:, 1024 + k:4096:16], ["VIx"], ["Xe%d" % k])
+                ts(T.OFF[:, o0 + m:o0 + 6:2], S[:, 18 * m + 15:18 * m + 18], S[:, 51 + 18 * m:52 + 18 * m],
+                   P["PB" + hs][:, 128 + m:129 + m], A.subtract, A.min, ["S" + hs, "PB" + hs], [ok[m]])
+            pick("v", Y[:, :], XW, T.OFF[:, o0:o0 + 6], ok + ["X" + hs, "Xp" + hs, "Xl" + hs, "Xr" + hs] + XI, ["Y" + hs])
+            ts(F1, T.OFF[:, o0:o0 + 2], PC[:, 9:10], None, A.subtract, None, ok + ["base"], [k1])
+            tt(DF, Y[:, 0:32], Y[:, 32:64], A.subtract, ["Y" + hs], ["DF" + hs])
+            for m in (0, 1):
+                tt(Z[:, 16 + 32 * m:32 + 32 * m], DF[:, 16 * m:16 * m + 16], Y[:, 64 + 16 * m:80 + 16 * m], A.add,
+                   ["Y" + hs, "DF" + hs], ["Z%d_%d" % (h, m)])
+            if last:
+                tt(T.DD[:, 4 * h:4 * h + 2], F0, F1, A.subtract, [k0, k1], ["DD" + hs])
             else:
-                send(T.MS[:, 48 * h:48 * h + 34], lambda s: T.FL[:, 144 * h + 48 * s:144 * h + 48 * s + 34],
-                     "af" + hs, ["NEW%d_%d" % (t, h), "MC" + hs])
-                arrive("af" + hs, allinc, ["LF" + hs])
-                mm(T["PA" + hs][:, 0:34], T.SB[:, 128 * h:128 * h + 128], T.CN[:, 0:34], True, False, SBK + ["CN"], ["PA" + hs])
-                for u in range(RO - 1):
-                    d0 = 40 * (2 * u + h)
-                    mm(T["PA" + hs][:, 0:34], T.ID[:, :], T.DL[:, d0:d0 + 34], False, False,
-                       ["ID", "DL%d_%d_0" % (u, h), "DL%d_%d_1" % (u, h)], ["PA" + hs])
-                labels(t, h, 0)
-                labels(t, h, 1)
-                d0 = 40 * (2 * t + h)
-                mm(T["PA" + hs][:, 0:34], T.ID[:, :], T.DL[:, d0:d0 + 34], False, True,
-                   ["ID", "DL%d_%d_0" % (t, h), "DL%d_%d_1" % (t, h)], ["PA" + hs])
-                update(t, h)
-                own(h)
+                places(h)
+                cap(t + 1, h)
+                put(XW, T.OFF[:, o0 + 2:o0 + 4], DF, Y[:, 64:96], ok + ["Y" + hs, "DF" + hs], ["X" + hs, "Xp" + hs, "Xl" + hs, "Xr" + hs])
+                for k, a, b in (("Xp", 0, 4), ("Xl", 3, 19), ("Xr", 20, 4)):
+                    cp("g", XW[:, a:BK:RW], XW[:, b:BK:RW], ["X" + hs], [k + hs])
+                mm(PS[:, 64:66], T.ID[:, :], F0, True, False, ["ID", k0], ["PS" + hs])
+                mm(PS[:, 64:66], T.NID[:, :], F1, False, True, ["NID", k1], ["PS" + hs])
+            labels(t, h, 0)
+            labels(t, h, 1)
+            turn(t, h, 0)
+            turn(t, h, 1)
+            out = T.MS[:, MW * h:MW * h + 34] if last else T.NS[:, 72 * t + 34 * h:72 * t + 34 * h + 34]
+            cp("v", out, PS[:, 0:34], ["PS" + hs], ["NS%d_%d" % (t, h)])
+            if last:
+                send(T.MS[:, MW * h:MW * h + 66], lambda s, h=h: T.FL[:, MW * (3 * h + s):MW * (3 * h + s) + 66],
+                     "af" + hs, ["NS%d_%d" % (t, h), "DL%d_%d_0" % (t, h), "DL%d_%d_1" % (t, h)], ["LF" + hs])
+                PW, c0, v0 = T["PW" + hs], 512 - MB, 3072 + 512 * h
+                for b in (0, 1):
+                    for m in (0, 1):
+                        mm(PW[:, c0 + MB * b:c0 + MB * b + MB], T.MV[:, 128 * (2 * m + b):128 * (2 * m + b) + 128], XW[:, MB * m:MB * m + MB],
+                           m == 0, m == 1, ["MV%d" % (2 * m + b), "X" + hs, "Xp" + hs, "Xl" + hs, "Xr" + hs], [("PA", "PB")[b] + hs])
+                for k in range(16):
+                    cp("s", T.VI[:, v0 + k:v0 + 512:16], PW[:, c0 + k + 4:c0 + BK:RW], ["PA" + hs, "PB" + hs], ["VP%d_%d" % (h, k)])
+                for b in (0, 1):
+                    ts(T.ON[:, 8 + 4 * h + b:9 + 4 * h + b], T.MS[:, MW * h + b:MW * h + b + 1], PC[:, 12:13], PC[:, 14 + b:15 + b], A.max, A.add,
+                       ["NS%d_%d" % (t, h)] + PKK, ["OM%d_%d" % (h, b)])
+                put(T.VI[:, v0:v0 + 512], T.ON[:, 8 + 4 * h:10 + 4 * h], T.MS[:, MW * h + 2:MW * h + 34], None,
+                    ["NS%d_%d" % (t, h), "OM%d_0" % h, "OM%d_1" % h] + ["VP%d_%d" % (h, k) for k in range(16)], ["B%d_3" % h])
+                block(3, h, "y", "out", ["B%d_3" % h], [])
+            elif h == 1:
+                send(T.NS[:, 72 * t:72 * t + 68], lambda s, t=t: T.VL[:, 204 * t + 68 * s:204 * t + 68 * s + 68], "ax%d" % t,
+                     ["NS%d_0" % t, "NS%d_1" % t], ["L%d" % t], NOM["slow"] if t < RO - 2 else None)
+                for t0, t1 in BATCH:
+                    if t1 == t + 1:
+                        offsets(t0, t1)
+            if t == RO - 2:
                 for m in (0, 1):
-                    c0, k0 = 64 * r + 32 * m + h, 40 * h + 18 * m
-                    tt(T.NL[:, c0:c0 + 31:2], T["PA" + hs][:, 18 * m:18 * m + 16], T.CAP[:, k0:k0 + 16], A.min,
-                       ["PA" + hs, "CAP" + hs], ["NL%d_%d" % (h, m)])
-            if (t, h) in JOBS:
-                j = JOBS[(t, h)]
-                apply(j, 0)
-                if last:
-                    apply(j, 1)
-                    fill.append(lambda: apply(RO - 2, 0, [0, 1]))
-                else:
-                    apply(j, 1, [0])
-                    fill.append(lambda j=j: apply(j, 1, [1, 2]))
+                    for w in range(RO - 1):
+                        d0 = 40 * (2 * w + h) + 18 * m
+                        mm(P["PA" + hs][:, 16 * m:16 * m + 16], T.ID[:, :], T.DL[:, d0:d0 + 16], w == 0, w == RO - 2,
+                           ["ID", "DL%d_%d_%d" % (w, h, m)], ["PA" + hs])
+                cp("v", T.DS[:, 64 * r + 32 * h:64 * r + 32 * h + 32], P["PA" + hs][:, 0:32], ["PA" + hs], ["DS" + hs])
+                if h == 1:
+                    send(T.DS[:, 64 * r:64 * r + 64], lambda s: T.DS[:, 64 * r:64 * r + 64], "an", ["DS0", "DS1"], ["DSx"])
 
-    NLK = ["NL0_0", "NL0_1", "NL1_0", "NL1_1"]
-    send(T.NL[:, 64 * r:64 * r + 64], lambda s: T.NL[:, 64 * r:64 * r + 64], "an", NLK)
-    arrive("an", allinc, ["NLx"])
-    apply(RO - 2, 0, [2])
-    apply(RO - 2, 1)
-    pack(range(0, 2), "g")
-    pack(range(2, 6), "s")
-    pack(range(6, 16), "v")
-    finish(0, "ys")
-    finish(1, "ys")
     for h in (0, 1):
-        mm(T["PB%d" % h][:, 0:128], T.NL[:, h:256:2], T.ID[:, :], True, True, NLK + ["NLx", "ID"], ["PB%d" % h])
-        ts(T.YI[:, 128 * h:128 * h + 128], T["PB%d" % h][:, 0:128], -1.0, None, A.add, None, ["PB%d" % h], ["YI%d" % h])
-    dma("y", "out", T.yi[:, :], T.YI[:, :], ["YI0", "YI1"], [])
+        finish(h, "ys" if h else "y")
+        slots(h, "y")
+    plan()
     need("g", [["c" + q, cnt[q], {}] for q in cnt] + list(grp.values()) + toks + [sent])

from concourse.bass import DstId, RemoteDMATransfer
from concourse.mybir import AluOpType as A, ActivationFunctionType as AF

RO = 6
NP = 2
RW = 21
BK = 32 * RW
MB = 16 * RW
KW = 70
MW = 72
CB = 64
CUT = {(t, h): (("s", 32), ("s", 32), ("v", 24), ("s", 40)) for t in range(RO) for h in (0, 1)}
CUT.update({(t, h): (("s", 32), ("s", 32), ("v", 20), ("s", 44)) for t in (3, 4) for h in (0, 1)})
CUT[0, 0] = (("s", 32), ("v", 32), ("s", 32), ("v", 32))
BATCH = ((0, 2), (2, 4), (4, 5))
DUE = {(3, 1): 2, (4, 0): 4, (4, 1): 6, (5, 0): 7, (5, 1): 9}
NOM = dict(cyc=1.0, pe=0.52, gat=1.3, sca=3.2, lat=40, self=70, wake=120, dma=60, rem=250, fly=1800, slow=3500, byte=0.005, turns=18,
           shake=300, tab=2500)
TOP = 557056.0
PEM = False
PLAN = {}

SCRATCH = {"ST": ("dram", [6, 128, 512], "bfloat16"), "LD": ("dram", [6, 128, 512], "bfloat16")}
for _d, _l in (("bfloat16", dict(TB=4096, G0=2048, G1=2048, X=2 * BK, VI=4096, WA=64, WR=128, WB=1024, ID=128, NID=128,
                                 ID16=128, MV=512, SW=256, IR=128, SEL=72, CK=72, CI=8, RC=8, RB=40, SB=256, F=64, DL=400,
                                 Y0=96, Y1=96, DF=64, Z0=80, Z1=80, NS=(RO - 1) * 72, VL=(RO - 1) * 204, DS=256, MS=2 * MW,
                                 FL=6 * MW, IB=256, CAP=256, SA=256, QB0=128, QB1=128)),
               ("float32", dict(DD=8, IOT=128, IOG=128, PC=32, GM=8, HA=72, HB=72, HC=72, HD=72, D0=72, YI=256, S0=72, S1=72)),
               ("int32", dict(PI=8, SI=256, SJ=256, IN=256, HI0=128, HI1=128, HJ0=128, HJ1=128)),
               ("uint16", dict(OFF=RO * 16, OP=(RO - 1) * 12, HO0=128, HO1=128, OF=16, ON=16))):
    for _n in _l:
        SCRATCH[_n] = ("sbuf", [128, _l[_n]], _d)
for _h in (0, 1):
    for _n, _w in (("PW", 1024), ("PK", 512), ("PS", 512)):
        SCRATCH["%s%d" % (_n, _h)] = ("psum", [128, _w], "float32")

SEMAPHORES = (["cv", "cs", "cp", "cg", "sent", "lw", "lsi", "lvo", "lvx", "lin", "tb", "aw", "an", "out"]
              + ["st%d" % k for k in range(NP)] + ["ad%d_%d" % (k, s) for k in range(NP) for s in range(3)]
              + ["ax%d" % t for t in range(RO - 1)] + ["af0", "af1"])


def lanes(topo, src, dsts):
    far = [d for d in dsts if topo.chip(d) != topo.chip(src)]
    near = [d for d in dsts if topo.chip(d) == topo.chip(src)]
    res = {}
    pool = topo.engines(src, far[0])
    n = len(pool) // len(far)
    for k, d in enumerate(far):
        res[d] = pool[k * n:(k + 1) * n]
    rest = [e for e in topo.engines(src, near[0]) if e not in pool]
    n = len(rest) // len(near)
    for k, d in enumerate(near):
        res[d] = rest[k * n:(k + 1) * n]
    return res


def rank_program(g, core, T, topo):
    r = T.rank_of(core)
    if r is None:
        return
    cores = list(T.cores)
    N = len(cores)
    peers = [(r + k) % N for k in range(1, N)]
    my = lanes(topo, core, [cores[p] for p in peers])
    inc = {p: len(lanes(topo, cores[p], [c for c in cores if c != cores[p]])[core]) for p in peers}
    allinc = sum(inc.values())
    far = [s for s in range(3) if topo.chip(cores[peers[s]]) != topo.chip(core)]
    near = [s for s in range(3) if s not in far][0]
    order = far + [near]

    Q = {"g": g, "v": g.vector, "s": g.scalar, "p": g.tensor, "y": g.sync}
    cnt = {"g": 0, "v": 0, "s": 0, "p": 0}
    clock = {q: {} for q in Q}
    lastw, readers, grp, toks = {}, {}, {}, []
    sent = ["sent", 0, {}]

    def merge(a, b):
        for k, x in b.items():
            if a.get(k, 0) < x:
                a[k] = x

    def need(q, ts):
        for tok in sorted(ts, key=lambda z: -z[1]):
            if clock[q].get(tok[0], 0) < tok[1]:
                Q[q].wait_ge(T.sem[tok[0]], tok[1])
                merge(clock[q], tok[2])
                clock[q][tok[0]] = tok[1]

    def deps(q, rd, wr, skip=None):
        ts = [lastw[k] for k in rd if k in lastw]
        for k in wr:
            if k[0] != "~":
                ts += ([lastw[k]] if k in lastw else []) + readers.get(k, [])
        need(q, [t for t in ts if t is not skip and not (q == "p" and t[0] == "cp")])

    def note(tok, rd, wr):
        for k in rd:
            readers.setdefault(k, []).append(tok)
        for k in wr:
            lastw[k] = tok
            readers[k] = []

    calls = []

    def op(q, fn, rd, wr, cost):
        def issue():
            deps(q, rd, wr)
            cnt[q] += 1
            fn().then_inc(T.sem["c" + q], 1)
            note(["c" + q, cnt[q], dict(clock[q])], rd, wr)
        calls.append((q, cost, NOM["lat"], rd, wr, None, issue))

    def dma(q, name, out, in_, rd, wr, lat=1500):
        def issue():
            tok = grp.setdefault(name, [name, 0, {}])
            deps(q, rd, wr, tok)
            Q[q].dma_start(out, in_).then_inc(T.sem[name], 16)
            tok[1] += 16
            merge(tok[2], clock[q])
            note(tok, rd, wr)
        if name == "out":
            calls.append((q, NOM["dma"], 0, rd, [">o%d" % len(calls)], name, issue))
            calls.append(("x", out.shape[0] * out.shape[1] * NOM["byte"], 1000, [">o%d" % (len(calls) - 1)], [], None, lambda: None))
        else:
            calls.append((q, NOM["dma"], lat, rd, wr, name, issue))

    def fused(items, rd, key):
        def issue():
            deps("g", rd, [])
            tr = []
            for s, eng, src, dst, sem in items:
                rid, pid = topo.addr(cores[peers[s]])[:2]
                there = (r - peers[s]) % N - 1
                tr.append(RemoteDMATransfer(dst_ids=[DstId(rid=rid, pnc=pid)], dma_engine_mask=sum(1 << e for e in eng),
                                            remote_sem=T.sem[sem(there)], src=src, dst=dst(there)))
                sent[1] += len(eng)
            g.remote_dma_fused(tr, local_sem=T.sem.sent)
        calls.append(("g", NOM["rem"], 0, rd, [key], "rem", issue))

    def arrive(sem, n, keys, key, lat):
        def issue():
            tok = [sem, n, {}]
            toks.append(tok)
            note(tok, [], keys)
        calls.append(("x", 1, lat, [key], keys, None, issue))

    def send(src, dst, sem, rd, keys, lat=None):
        fused([(s, my[cores[peers[s]]], src, dst, lambda x: sem) for s in order], rd, ">" + sem)
        arrive(sem, allinc, keys, ">" + sem, lat or NOM["fly"])

    def plan():
        n, w, rs, pred, fifo = len(calls), {}, {}, [], {}
        for j, (q, cost, lat, rd, wr, gp, fn) in enumerate(calls):
            e = {}
            for i in [i for k in rd + wr if k[0] != "~" for i in w.get(k, [])] + [i for k in wr for i in rs.get(k, [])]:
                if gp is None or calls[i][5] != gp:
                    a = calls[i]
                    e[i] = a[1] + (0 if a[0] == q == "p" or q == "x" else a[2] + NOM["self" if a[0] == q and not a[5] else "wake"])
            for i in [i for k in wr if k[0] == "~" for i in w.get(k, [])]:
                e.setdefault(i, calls[i][1])
            if gp:
                if q in fifo:
                    e.setdefault(fifo[q], calls[fifo[q]][1])
                fifo[q] = j
            pred.append(e)
            for k in rd:
                rs.setdefault(k, []).append(j)
            for k in wr:
                w[k] = [i for i in w.get(k, []) if gp and calls[i][5] == gp] + [j]
                rs[k] = []
        tail = [c[1] + c[2] for c in calls]
        for j in range(n - 1, -1, -1):
            for i, d in pred[j].items():
                tail[i] = max(tail[i], d + tail[j])
        succ = [{} for c in calls]
        for j in range(n):
            for i, d in pred[j].items():
                succ[i][j] = d - calls[i][1] + calls[j][1]

        def fit(rank, before, first):
            start, busy = [0] * n, {}
            for j in sorted(range(n), key=lambda j: rank[j]):
                q, cost = calls[j][:2]
                t = max([start[i] + d for i, d in before[j].items()] + [first[j]])
                line = busy.setdefault(q, [])
                k = len(line)
                while k and line[k - 1][1] > t:
                    k -= 1
                while k < len(line) and line[k][0] < t + cost:
                    t = max(t, line[k][1])
                    k += 1
                line.insert(k, (t, t + cost))
                start[j] = t
            return start

        def order(rank, before):
            for j in (range(n) if before is pred else range(n - 1, -1, -1)):
                for i in before[j]:
                    rank[j] = max(rank[j], rank[i] + 0.001)
            return rank

        start, best, z = fit([-x for x in tail], pred, [0] * n), PLAN.get(r), [1]

        def noise(a):
            z[0] = z[0] * 48271 % 2147483647
            return a * (z[0] / 2147483647.0 - 0.5)

        for k in range(0 if best else NOM["turns"]):
            end = max(start[j] + calls[j][1] + calls[j][2] for j in range(n))
            if best is None or end < best[0]:
                best = (end, start)
            a = NOM["shake"] if k % 3 == 2 else 0
            if a:
                start = best[1]
            back = fit(order([-start[j] - calls[j][1] + noise(a) for j in range(n)], succ), succ, [c[2] for c in calls])
            start = fit([-back[j] - calls[j][1] for j in range(n)], pred, [0] * n)
        PLAN[r] = best
        for j in sorted(range(n), key=lambda j: (best[1][j], j)):
            calls[j][6]()

    V = g.vector

    def cyc(out, *ins):
        two = all("16" in str(a.dtype) for a in (out,) + ins)
        return NOM["cyc"] * max(64, out.shape[1] * (0.5 if two else 1))

    def ts(out, in0, s1, s2, o0, o1, rd, wr):
        if o1 is None:
            op("v", lambda: V.tensor_scalar(out, in0, s1, None, o0), rd, wr, cyc(out, in0))
        else:
            op("v", lambda: V.tensor_scalar(out, in0, s1, s2, o0, o1), rd, wr, cyc(out, in0))

    def tt(out, a, b, o, rd, wr):
        op("v", lambda: V.tensor_tensor(out, a, b, o), rd, wr, NOM["cyc"] * max(64, 2 * out.shape[1]))

    def cp(q, out, in_, rd, wr):
        n = out.shape[1]
        if q == "v":
            op(q, lambda: V.tensor_copy(out, in_), rd, wr, cyc(out, in_))
        elif q == "s":
            op(q, lambda: g.scalar.activation(out, in_, AF.Copy), rd, wr, NOM["cyc"] * max(64, n))
        else:
            op(q, lambda: g.affine_select(out, in_, [[0, n]], A.is_equal, 0.0, 0, 0), rd, wr, 170 + 2 * n * NOM["cyc"])

    def pick(q, out, win, off, rd, wr):
        cost = 60 + NOM["gat"] * out.shape[1]
        if q == "v":
            op(q, lambda: V.tensor_copy(out, win.indirect(off)), rd, wr, cost)
        else:
            op(q, lambda: g.scalar.activation(out, win.indirect(off), AF.Copy), rd, wr + ["~s"], cost)

    def put(win, off, a, b, rd, wr):
        cost = 50 + NOM["sca"] * a.shape[1]
        if b is None:
            op("v", lambda: V.tensor_copy(win.indirect(off), a), rd, wr, cost)
        else:
            op("v", lambda: V.tensor_tensor(win.indirect(off), a, b, A.add), rd, wr, cost)

    def ms(out, val, wr):
        op("v", lambda: V.memset(out, val), [], wr, cyc(out))

    def mm(out, lhsT, rhs, start, stop, rd, wr):
        op("p", lambda: g.tensor.matmul(out, lhsT, rhs, start, stop), rd, wr, NOM["pe"] * max(min(64, out.shape[0]), out.shape[1]))

    def iota(out, pattern, channel, wr):
        fl = {} if "int" in str(out.dtype) else {"allow_small_or_imprecise_dtypes": True}
        op("g", lambda: g.iota(out, pattern, 0, channel, **fl), [], wr, 130 + 2 * out.shape[1] * NOM["cyc"])

    def scan(t, h):
        S, PK = T["S%d" % h], T["PK%d" % h]
        op("v", lambda: V.tensor_tensor_scan(S[:, 0:KW], T.D0[:, 0:KW], PK[:, 0:KW], 0.0, A.add, A.max), ["D0", "PK%d" % h],
           ["S%d" % h] + ["~a%d" % k for k in range(DUE.get((t, h), 0))], NOM["cyc"] * KW)

    R0 = 32 * r

    P = {}
    for h in (0, 1):
        P.update({"PA%d" % h: T["PW%d" % h][:, 0:512], "PB%d" % h: T["PW%d" % h][:, 512:1024]})

    def block(s, h, qs, sem, rd, wr, lat=1500):
        d, v0 = 32 * (peers + [r])[s], 1024 * s + 512 * h
        for t in range(4):
            c0, sb = 2048 * h + 512 * t, T.VI[32 * t:32 * t + 32, v0:v0 + 512]
            if sem == "out":
                dma(qs[t % len(qs)], sem, T.yv[d:d + 32, c0:c0 + 512], sb, rd, wr)
            else:
                dma(qs[t % len(qs)], sem, sb, T.v[d:d + 32, c0:c0 + 512], rd, wr, lat)

    dma("y", "lw", T.WA[:, 16 * r:16 * r + 16], T.wt[:, :], [], ["WAo"], 1200)
    for q, s, k, c in (("s", far[0], 0, 0), ("y", far[1], 0, 0), ("s", far[0], 1, 1), ("y", far[1], 1, 1),
                       ("s", near, 0, 1), ("y", near, 1, 1)):
        d = 32 * peers[s] + 16 * k
        dma(q, "st%d" % c, T.ST[2 * s + k], T.dem[d:d + 16, :], [], ["ST%d" % c], 1700 + 1200 * c)
    dma("s", "lsi", T.SI[64:96, :], T.inv[R0:R0 + 32, :], [], ["SI"], 2800)
    dma("s", "lsi", T.SI[0:32, :], T.sup[R0:R0 + 32, :], [], ["SI"], 2800)
    dma("y", "lsi", T.SI[32:64, :], T.sup[R0:R0 + 32, :], [], ["SI"], 2800)
    for h in (0, 1):
        block(3, h, "ys", "lvo", [], ["VIo"], 3000)
    dma("y", "lin", T.IN[:, :], T.inv[:, :], [], ["IN"], 3000)
    for m in (0, 1):
        d = 64 * m + 16 * r
        dma("y", "tb", T.TB[d:d + 16, :], T.dem[R0 + 16 * m:R0 + 16 * m + 16, :], ["ST1"], ["TB"])

    iota(T.PI[:, 0:1], [[0, 1]], 1, ["PI0"])
    iota(T.IOT[:, :], [[1, 128]], 0, ["IOT"])
    iota(T.IOG[:, :], [[0, 8], [1, 16]], 0, ["IOG"])
    send(T.WA[:, 16 * r:16 * r + 16], lambda s: T.WA[:, 16 * r:16 * r + 16], "aw", ["WAo"], ["WAx"], 3000)

    def piece(s, k, eng):
        return (s, eng, T.ST[2 * s + k], lambda x: T.LD[2 * x + k], lambda x: "ad%d_%d" % (k, x))

    en = my[cores[peers[near]]]
    fused([piece(s, 0, my[cores[peers[s]]]) for s in far], ["ST0"], ">t0")
    fused([piece(s, 1, my[cores[peers[s]]]) for s in far]
          + [piece(near, 0, en[:len(en) // 2]), piece(near, 1, en[len(en) // 2:])], ["ST1"], ">t1")
    for q, s, k in (("y", far[0], 0), ("y", far[1], 0), ("y", near, 0), ("y", near, 1), ("y", far[0], 1), ("y", far[1], 1)):
        key = "ad%d_%d" % (k, s)
        arrive(key, inc[peers[s]] // (2 if s == near else 1), [key], ">t%d" % (k or s == near), NOM["tab"])
        d = 64 * k + 16 * peers[s]
        dma(q, "tb", T.TB[d:d + 16, :], T.LD[2 * s + k], [key], ["TB"])
    for h in (0, 1):
        for s in range(3):
            block(s, h, "y", "lvx", ["TB"], ["VIx"])

    PC = T.PC
    ts(T.PI[:, 1:2], T.PI[:, 0:1], 4, 1, A.arith_shift_right, A.bitwise_and, ["PI0"], ["PI1"])
    ts(T.PI[:, 2:3], T.PI[:, 0:1], 15, None, A.bitwise_and, None, ["PI0"], ["PI2"])
    ts(T.PI[:, 3:4], T.PI[:, 0:1], 6, None, A.arith_shift_right, None, ["PI0"], ["PI3"])
    ts(T.PI[:, 4:5], T.PI[:, 0:1], 4, None, A.arith_shift_right, None, ["PI0"], ["PI4"])
    cp("v", PC[:, 0:5], T.PI[:, 0:5], ["PI0", "PI1", "PI2", "PI3", "PI4"], ["PC"])
    p_, pm, pi, tm, gr = [PC[:, k:k + 1] for k in range(5)]
    ms(T.D0[:, :], 0.0, ["D0"])
    ms(T.D0[:, 0:55:18], -67108864.0, ["D0"])
    ms(T.D0[:, 16:18], 1.0, ["D0"])
    ms(T.D0[:, 34:36], 1.0, ["D0"])
    ms(T.DL[:, :], 0.0, ["DLz"])
    ms(T.Z0[:, :], 0.0, ["Z0z"])
    ms(T.Z1[:, :], 0.0, ["Z1z"])
    ms(T.X[:, 1:2 * BK:RW], 100.0, ["Xk1"])
    ms(T.X[:, 2:2 * BK:RW], 100.0, ["Xk2"])
    cp("v", T.IR[0:32, :], T.IOG[0:32, :], ["IOG"], ["IR0"])
    ms(T.IR[32:64, :], 1.0, ["IR1"])
    ms(T.RC[0:32, 0:2], RW / 32.0, ["RC0"])
    ms(T.RC[32:64, 0:1], 8.0 * MB / 32, ["RC1"])
    ms(T.RC[32:64, 1:2], -7.0 * MB / 32, ["RC2"])
    ms(T.RB[0:32, :], -RW / 32.0, ["RB0"])
    ms(T.RB[32:64, 0:18], 0.0, ["RB1"])
    ms(T.RB[32:64, 18:36], -MB / 32.0, ["RB2"])
    IRK = ["IR0", "IR1"]
    ts(PC[:, 5:6], pm, 1000.0, p_, A.mult, A.add, ["PC"], ["ca"])
    ts(PC[:, 6:7], pm, -1000.0, p_, A.mult, A.add, ["PC"], ["cb"])
    ts(PC[:, 7:8], pm, 18.0, pi, A.mult, A.add, ["PC"], ["cA"])
    ts(PC[:, 8:9], tm, 18.0, pi, A.mult, A.add, ["PC"], ["cT"])
    ts(PC[:, 9:10], pi, float(RW), MB / 2.0, A.mult, A.add, ["PC"], ["base"])
    ca, cb = PC[:, 5:6], PC[:, 6:7]
    for m in (0, 1):
        ts(T.SW[:, 128 * m:128 * m + 128], T.IOG[:, :], R0 + 16.0 * m, p_, A.add, A.is_equal, ["IOG", "PC"], ["SW%d" % m])
    ts(T.CI[:, 0:2], T.IOT[:, 4:6], gr, -1.0, A.is_equal, A.mult, ["IOT", "PC"], ["CI"])
    ts(T.GM[:, :], T.IOT[:, 0:8], gr, None, A.is_equal, None, ["IOT", "PC"], ["GM"])
    ts(T.ID[:, :], T.IOT[:, :], p_, None, A.is_equal, None, ["IOT", "PC"], ["ID"])
    ts(T.ID16[:, :], T.IOT[:, :], p_, 16.0, A.is_equal, A.mult, ["IOT", "PC"], ["ID16"])
    ts(T.NID[:, :], T.IOT[:, :], p_, -1.0, A.is_equal, A.mult, ["IOT", "PC"], ["NID"])
    ts(T.MV[:, 0:128], T.IOT[:, :], ca, None, A.is_equal, None, ["IOT", "ca"], ["MV0"])
    ts(T.MV[:, 128:256], T.IOT[:, :], -984.0, cb, A.add, A.is_equal, ["IOT", "cb"], ["MV1"])
    ts(T.MV[:, 256:384], T.IOT[:, :], -16.0, ca, A.add, A.is_equal, ["IOT", "ca"], ["MV2"])
    ts(T.MV[:, 384:512], T.IOT[:, :], -1000.0, cb, A.add, A.is_equal, ["IOT", "cb"], ["MV3"])
    ms(T.SB[96:128, :], 1.0, ["SB3"])
    ts(T.SA[64:96, :], T.SI[64:96, :], 0.0, 2.0, A.is_ge, A.mult, ["SI"], ["SA"])
    ts(T.SB[64:96, :], T.SI[64:96, :], 1.0, None, A.add, None, ["SI"], ["SB2"])
    tt(T.SB[64:96, :], T.SB[64:96, :], T.SA[64:96, :], A.add, ["SA", "SB2"], ["SB2"])
    ts(T.SJ[0:32, :], T.SI[0:32, :], 7, None, A.arith_shift_right, None, ["SI"], ["SJ0"])
    ts(T.SJ[32:64, :], T.SI[32:64, :], 127, None, A.bitwise_and, None, ["SI"], ["SJ1"])
    cp("v", T.SB[0:64, :], T.SJ[0:64, :], ["SJ0", "SJ1"], ["SB0"])
    SBK = ["SB0", "SB2", "SB3"]
    ms(PC[0:32, 10:12], -65536.0, ["sa0"])
    ms(PC[32:64, 10:12], -512.0, ["sa1"])
    ms(PC[64:96, 10:11], 1.0, ["sa2"])
    ms(PC[64:96, 11:12], 0.0, ["sa2b"])
    ts(PC[96:128, 10:11], PC[96:128, 2:3], -32.0, 480.0, A.mult, A.add, ["PC"], ["sa3"])
    ts(PC[96:128, 11:12], PC[96:128, 2:3], -32.0, 480.0, A.mult, A.add, ["PC"], ["sa3b"])
    sas = ["sa0", "sa1", "sa2", "sa2b", "sa3", "sa3b"]
    ts(T.HA[:, :], T.IOT[:, 0:72], PC[:, 7:8], PC[:, 10:11], A.is_equal, A.mult, ["IOT", "cA"] + sas, ["HA"])
    ts(T.HB[:, :], T.IOT[:, 0:72], -36.0, PC[:, 7:8], A.add, A.is_equal, ["IOT", "cA"], ["HB"])
    ts(T.HB[:, :], T.HB[:, :], PC[:, 11:12], None, A.mult, None, ["HB"] + sas, ["HB"])
    tt(T.CK[:, :], T.HA[:, :], T.HB[:, :], A.add, ["HA", "HB"], ["CK"])
    ms(T.CK[96:128, 16:18], -1048576.0, ["CK"])
    ms(T.CK[96:128, 34:36], -1048576.0, ["CK"])
    ts(T.HC[:, :], T.IOT[:, 0:72], PC[:, 8:9], 512.0, A.is_equal, A.mult, ["IOT", "cT"], ["HC"])
    cp("v", T.SEL[:, 0:36], T.HC[:, 0:36], ["HC"], ["SEL0"])
    cp("v", T.SEL[:, 36:72], T.HC[:, 0:36], ["HC"], ["SEL1"])
    ts(PC[:, 12:13], pm, float(MB), 3.0 - MB / 2, A.mult, A.add, ["PC"], ["pk0"])
    ts(PC[:, 13:14], pi, 16.0, PC[:, 12:13], A.mult, A.subtract, ["PC", "pk0"], ["pk1"])
    for k in range(4):
        ts(PC[:, 14 + k:15 + k], PC[:, 13:14], 256.0 * k, None, A.add, None, ["pk1"], ["pk%d" % (2 + k)])
    PKK = ["pk%d" % k for k in range(6)]
    cp("v", T.IB[:, :], T.IN[:, :], ["IN"], ["IB"])
    ts(T.CAP[:, :], T.IN[:, :], 16.0, 15.0, A.mult, A.add, ["IN"], ["CAP"])
    for x in range(N):
        for m in (0, 1):
            mm(T.PK0[:, 64 * m + 16 * x:64 * m + 16 * x + 16], T.SW[:, 128 * m:128 * m + 128], T.WA[:, 16 * x:16 * x + 16],
               True, True, ["SW%d" % m, "WAo", "WAx"], ["PK0"])
    cp("v", T.WR[:, :], T.PK0[:, 0:128], ["PK0"], ["WR"])
    for k in range(8):
        ts(T.WB[:, k:1024:8], T.WR[:, :], T.GM[:, k:k + 1], None, A.mult, None, ["WR", "GM"], ["WB%d" % k])
    WBK = ["WB%d" % k for k in range(8)]
    for h in (0, 1):
        for m in (0, 1):
            for b in (0, 1):
                c0 = 3072 + 512 * h + 256 * b
                mm(T.PW0[:, 512 * h + 256 * m:512 * h + 256 * m + 256], T.MV[:, 128 * (2 * b + m):128 * (2 * b + m) + 128],
                   T.VI[:, c0:c0 + 256], b == 0, b == 1, ["MV%d" % (2 * b + m), "VIo"], [("PA0", "PB0")[h]])
    for k, a in [(k + 4, k) for k in range(16)] + [(0, 0), (3, 15), (20, 0)]:
        cp("s", T.X[:, k:2 * BK:RW], T.PW0[:, a:1024:16], ["PA0", "PB0"], ["Xi%d" % k])
    XI = ["Xk1", "Xk2"] + ["Xi%d" % k for k in [0] + list(range(3, RW))]

    def rel(t, h):
        return T.F[:, 8 * t + 4 * h:8 * t + 4 * h + 2], "F%d_%d" % (t, h)

    def cap(t, h):
        Fap, fk = rel(t, h)
        mm(P["PB%d" % h][:, 128:130], T.IR[0:64, :], T.RC[0:64, 0:2], True, False, IRK + ["RC0", "RC1", "RC2"], ["PB%d" % h])
        mm(P["PB%d" % h][:, 128:130], T.ID16[:, :], Fap, False, True, ["ID16", fk], ["PB%d" % h])

    def places(h):
        hs, Z = str(h), T["Z%d" % h]
        for c, (bank, a, b) in enumerate((("PA" + hs, 0, CB), ("PB" + hs, CB, 128))):
            for m in (0, 1):
                for x in range(N):
                    p0, z0, w0 = 64 * m + 32 * (x // 2), 32 * m + 16 * (1 - x % 2), 128 * (4 * m + x)
                    mm(P[bank][p0:p0 + 32, 0:b - a], Z[:, z0:z0 + 32], T.WB[:, w0 + a:w0 + b], m + x == 0 if PEM else x % 2 == 0, x % 2 == 1,
                       WBK + ["Z%d_%d" % (h, m), "Z%dz" % h], [bank])
            key = hs + str(c)
            if PEM:
                ts(T["QB" + hs][:, a:b], P[bank][:, 0:b - a], TOP - 2047.5, None, A.add, None, [bank], ["QB" + key])
                mm(P[bank][:, 0:b - a], T.NID[:, :], T["QB" + hs][:, a:b], False, True, ["NID", "QB" + key], [bank])
                ts(T["HO" + hs][:, a:b], P[bank][:, 0:b - a], TOP, None, A.add, None, [bank], ["HO" + key])
                continue
            cp("v", T["HI" + hs][:, a:b], P[bank][:, 0:b - a], [bank], ["HI" + key])
            ts(T["HJ" + hs][:, a:b], T["HI" + hs][:, a:b], 4095, None, A.bitwise_and, None, ["HI" + key], ["HJ" + key])
            cp("v", T["HO" + hs][:, a:b], T["HJ" + hs][:, a:b], ["HJ" + key], ["HO" + key])

    def keys(t, h):
        hs = str(h)
        PK = T["PK" + hs]
        mm(PK[:, 0:KW], T.SB[:, 128 * h:128 * h + 128], T.CK[:, 0:KW], True, False, SBK + ["CK"], ["PK" + hs])
        mm(PK[:, 36:KW], T.IR[0:64, :], T.RB[0:64, 0:34], False, False, IRK + ["RB0", "RB1", "RB2"], ["PK" + hs])
        for u in range(t):
            d0 = 40 * (2 * u + h)
            mm(PK[:, 0:34], T.ID[:, :], T.DL[:, d0:d0 + 34], False, False,
               ["ID", "DLz", "DL%d_%d_0" % (u, h), "DL%d_%d_1" % (u, h)], ["PK" + hs])
        a, ends = 0, []
        for q, n in CUT[t, h]:
            pick(q, T["G" + hs][:, 16 * a:16 * (a + n)], T.TB[:, :], T["HO" + hs][:, a:a + n],
                 ["TB"] + ["HO%s%d" % (hs, c) for c in {a >= CB, a + n > CB}], ["G%s_%d" % (hs, c) for c in range(a // 4, (a + n) // 4)])
            a += n
        for e in range(16):
            mm(PK[:, 0:KW], T["G" + hs][:, 128 * e:128 * e + 128], T.SEL[:, 0:KW], False, e == 15,
               ["G%s_%d" % (hs, 2 * e), "G%s_%d" % (hs, 2 * e + 1), "SEL0", "SEL1"], ["PK" + hs])

    def labels(t, h, m):
        hs = str(h)
        if t < RO - 1:
            d0 = 40 * (2 * t + h) + 18 * m
            out, dd, k = T.DL[:, d0:d0 + 16], T["PS" + hs][:, 64 + m:65 + m], "PS" + hs
        else:
            d0 = MW * h + 34 + 16 * m
            out, dd, k = T.MS[:, d0:d0 + 16], T.DD[:, 4 * h + m:4 * h + m + 1], "DD" + hs
        ts(out, T["PK" + hs][:, 18 * m:18 * m + 16], T["S" + hs][:, 18 * m + 15:18 * m + 16], dd, A.is_equal, A.mult,
           ["PK" + hs, "S" + hs, k, "DLz"], ["DL%d_%d_%d" % (t, h, m)])

    def turn(t, h, what):
        hs = str(h)
        Fap, fk = rel(t + 1, h)
        first = h == 0 or t == RO - 1
        for b in (0, 1):
            for m in (0, 1):
                if what:
                    c0, n, src, k = 16 * b + (2 if first else 0), 16, T["Z" + hs][:, 16 + 32 * m:32 + 32 * m], "Z%d_%d" % (h, m)
                else:
                    c0, n, src, k = b + (0 if first else 32), 1, Fap[:, m:m + 1], fk
                mm(T["PS" + hs][:, c0:c0 + n], T.MV[:, 128 * (2 * m + b):128 * (2 * m + b) + 128], src, m == 0, m == 1,
                   ["MV%d" % (2 * m + b), k], ["PS" + hs])

    def offsets(t0, t1):
        for h in (0, 1):
            for b in (0, 1):
                ts(T.OP[:, 12 * t0 + 2 * h + b:12 * t1:4], T.VL[:, 204 * t0 + 66 * h + b:204 * t1:68],
                   PC[:, 12:13], PC[:, 14 + 2 * h + b:15 + 2 * h + b], A.max, A.add,
                   PKK + ["L%d" % t for t in range(t0, t1)], ["OP%d_%d%d" % (t, h, b) for t in range(t0, t1)])
        for t in range(t0, t1):
            for s in range(3):
                put(T.VI[:, 1024 * s:1024 + 1024 * s], T.OP[:, 12 * t + 4 * s:12 * t + 4 * s + 4],
                    T.VL[:, 204 * t + 68 * s + 2:204 * t + 68 * s + 66], None,
                    ["L%d" % t, "VIx"] + ["OP%d_%d%d" % (t, h, b) for h in (0, 1) for b in (0, 1)], ["B0_%d" % s, "B1_%d" % s, "~a%d" % (3 * t + s)])

    def finish(h, qs):
        hs = str(h)
        for b in (0, 1):
            ts(T.OF[:, 8 * h + b:8 * h + 6:2], T.FL[:, 3 * MW * h + b:3 * MW * (h + 1):MW], PC[:, 12:13], PC[:, 14 + b:15 + b], A.max, A.add,
               ["LF" + hs] + PKK, ["OF%d_%d" % (h, b)])
        for s in range(3):
            v0, f0 = 1024 * s + 512 * h, MW * (3 * h + s) + 2
            put(T.VI[:, v0:v0 + 512], T.OF[:, 8 * h + 2 * s:8 * h + 2 * s + 2], T.FL[:, f0:f0 + 32], None,
                ["LF" + hs, "OF%d_0" % h, "OF%d_1" % h], ["B%d_%d" % (h, s)])
            block(s, h, qs, "out", ["B%d_%d" % (h, s)], [])

    def slots(h, q):
        hs = str(h)
        PB = T["PK" + hs]
        mm(PB[:, 0:128], T.ID[:, :], T.IB[:, 128 * h:128 * h + 128], True, False, ["ID", "IB"], ["PK" + hs])
        for x in range(N):
            mm(PB[32 * x:32 * x + 32, 0:128], T.DS[:, 64 * x + 32 * h:64 * x + 32 * h + 32], T.ID[:, :], False, False,
               ["ID", "DS0", "DS1", "DSx"], ["PK" + hs])
        for k, x in enumerate([r] + peers):
            src = T.MS[:, MW * h + 34:MW * h + 66] if k == 0 else T.FL[:, MW * (3 * h + k - 1) + 34:MW * (3 * h + k - 1) + 66]
            mm(PB[32 * x:32 * x + 32, 0:128], src, T.ID[:, :], False, True,
               ["ID", "DL%d_%d_0" % (RO - 1, h), "DL%d_%d_1" % (RO - 1, h)] + (["LF" + hs] if k else []), ["PK" + hs])
        tt(T.YI[:, 128 * h:128 * h + 128], PB[:, 0:128], T.CAP[:, 128 * h:128 * h + 128], A.min, ["PK" + hs, "CAP"], ["YI" + hs])
        dma(q, "out", T.yi[:, 128 * h:128 * h + 128], T.YI[:, 128 * h:128 * h + 128], ["YI" + hs], [])

    for h in (0, 1):
        hs = str(h)
        mm(T["PS" + hs][:, 0:2], T.SB[64:96, 128 * h:128 * h + 128], T.CI[64:96, 0:2], True, True, ["SB2", "CI"], ["PS" + hs])
        for m in (0, 1):
            ts(T.ON[:, 4 * h + 2 * m:4 * h + 2 * m + 1], T["PS" + hs][:, m:m + 1], PC[:, 9:10], 169.0 + MB * m - MB / 2, A.add, A.add,
               ["PS" + hs, "base"], ["ON%d_%d" % (h, m)])
            pick("v", T["Z" + hs][:, 16 + 32 * m:32 + 32 * m], T.X[:, BK * h:BK * h + BK], T.ON[:, 4 * h + 2 * m:4 * h + 2 * m + 1],
                 ["ON%d_%d" % (h, m), "Z%dz" % h] + XI, ["Z%d_%d" % (h, m)])
            ts(T.F[:, 4 * h + m:4 * h + m + 1], T["PS" + hs][:, m:m + 1], 168.0 + MB * m - MB / 2, None, A.add, None,
               ["PS" + hs], ["F0_" + hs])
        places(h)
        cap(0, h)

    for t in range(RO):
        last = t == RO - 1
        for h in (0, 1):
            hs = str(h)
            PS, S, Y, Z = T["PS" + hs], T["S" + hs], T["Y" + hs], T["Z" + hs]
            DF, XW = T.DF[:, 32 * h:32 * h + 32], T.X[:, BK * h:BK * h + BK]
            o0, ok = 16 * t + 6 * h, ["OFF%d_%d_%d" % (t, h, m) for m in (0, 1)]
            (F0, k0), (F1, k1) = rel(t, h), rel(t + 1, h)
            keys(t, h)
            scan(t, h)
            for m in (0, 1):
                ts(T.OFF[:, o0 + m:o0 + 6:2], S[:, 18 * m + 15:18 * m + 18], S[:, 51 + 18 * m:52 + 18 * m],
                   P["PB" + hs][:, 128 + m:129 + m], A.subtract, A.min, ["S" + hs, "PB" + hs], [ok[m]])
            pick("v", Y[:, :], XW, T.OFF[:, o0:o0 + 6], ok + ["X" + hs, "Xp" + hs, "Xl" + hs, "Xr" + hs] + XI, ["Y" + hs])
            ts(F1, T.OFF[:, o0:o0 + 2], PC[:, 9:10], None, A.subtract, None, ok + ["base"], [k1])
            tt(DF, Y[:, 0:32], Y[:, 32:64], A.subtract, ["Y" + hs], ["DF" + hs])
            for m in (0, 1):
                tt(Z[:, 16 + 32 * m:32 + 32 * m], DF[:, 16 * m:16 * m + 16], Y[:, 64 + 16 * m:80 + 16 * m], A.add,
                   ["Y" + hs, "DF" + hs], ["Z%d_%d" % (h, m)])
            if last:
                tt(T.DD[:, 4 * h:4 * h + 2], F0, F1, A.subtract, [k0, k1], ["DD" + hs])
            else:
                places(h)
                cap(t + 1, h)
                put(XW, T.OFF[:, o0 + 2:o0 + 4], DF, Y[:, 64:96], ok + ["Y" + hs, "DF" + hs], ["X" + hs, "Xp" + hs, "Xl" + hs, "Xr" + hs])
                for k, a, b in (("Xp", 0, 4), ("Xl", 3, 19), ("Xr", 20, 4)):
                    cp("g", XW[:, a:BK:RW], XW[:, b:BK:RW], ["X" + hs], [k + hs])
                mm(PS[:, 64:66], T.ID[:, :], F0, True, False, ["ID", k0], ["PS" + hs])
                mm(PS[:, 64:66], T.NID[:, :], F1, False, True, ["NID", k1], ["PS" + hs])
            labels(t, h, 0)
            labels(t, h, 1)
            turn(t, h, 0)
            turn(t, h, 1)
            out = T.MS[:, MW * h:MW * h + 34] if last else T.NS[:, 72 * t + 34 * h:72 * t + 34 * h + 34]
            cp("v", out, PS[:, 0:34], ["PS" + hs], ["NS%d_%d" % (t, h)])
            if last:
                send(T.MS[:, MW * h:MW * h + 66], lambda s, h=h: T.FL[:, MW * (3 * h + s):MW * (3 * h + s) + 66],
                     "af" + hs, ["NS%d_%d" % (t, h), "DL%d_%d_0" % (t, h), "DL%d_%d_1" % (t, h)], ["LF" + hs])
                PW, c0, v0 = T["PW" + hs], 512 - MB, 3072 + 512 * h
                for b in (0, 1):
                    for m in (0, 1):
                        mm(PW[:, c0 + MB * b:c0 + MB * b + MB], T.MV[:, 128 * (2 * m + b):128 * (2 * m + b) + 128], XW[:, MB * m:MB * m + MB],
                           m == 0, m == 1, ["MV%d" % (2 * m + b), "X" + hs, "Xp" + hs, "Xl" + hs, "Xr" + hs], [("PA", "PB")[b] + hs])
                for k in range(16):
                    cp("s", T.VI[:, v0 + k:v0 + 512:16], PW[:, c0 + k + 4:c0 + BK:RW], ["PA" + hs, "PB" + hs], ["VP%d_%d" % (h, k)])
                for b in (0, 1):
                    ts(T.ON[:, 8 + 4 * h + b:9 + 4 * h + b], T.MS[:, MW * h + b:MW * h + b + 1], PC[:, 12:13], PC[:, 14 + b:15 + b], A.max, A.add,
                       ["NS%d_%d" % (t, h)] + PKK, ["OM%d_%d" % (h, b)])
                put(T.VI[:, v0:v0 + 512], T.ON[:, 8 + 4 * h:10 + 4 * h], T.MS[:, MW * h + 2:MW * h + 34], None,
                    ["NS%d_%d" % (t, h), "OM%d_0" % h, "OM%d_1" % h] + ["VP%d_%d" % (h, k) for k in range(16)], ["B%d_3" % h])
                block(3, h, "y", "out", ["B%d_3" % h], [])
            elif h == 1:
                send(T.NS[:, 72 * t:72 * t + 68], lambda s, t=t: T.VL[:, 204 * t + 68 * s:204 * t + 68 * s + 68], "ax%d" % t,
                     ["NS%d_0" % t, "NS%d_1" % t], ["L%d" % t], NOM["slow"] if t < RO - 2 else None)
                for t0, t1 in BATCH:
                    if t1 == t + 1:
                        offsets(t0, t1)
            if t == RO - 2:
                for m in (0, 1):
                    for w in range(RO - 1):
                        d0 = 40 * (2 * w + h) + 18 * m
                        mm(P["PA" + hs][:, 16 * m:16 * m + 16], T.ID[:, :], T.DL[:, d0:d0 + 16], w == 0, w == RO - 2,
                           ["ID", "DL%d_%d_%d" % (w, h, m)], ["PA" + hs])
                cp("v", T.DS[:, 64 * r + 32 * h:64 * r + 32 * h + 32], P["PA" + hs][:, 0:32], ["PA" + hs], ["DS" + hs])
                if h == 1:
                    send(T.DS[:, 64 * r:64 * r + 64], lambda s: T.DS[:, 64 * r:64 * r + 64], "an", ["DS0", "DS1"], ["DSx"])

    for h in (0, 1):
        finish(h, "ys" if h else "y")
        slots(h, "y")
    plan()
    need("g", [["c" + q, cnt[q], {}] for q in cnt] + list(grp.values()) + toks + [sent])
